import numpy as np
import ml_dtypes


def mxq(x, axis, fmt="e4m3"):
    dtype, down = {"e4m3": (ml_dtypes.float8_e4m3fn, 7), "e5m2": (ml_dtypes.float8_e5m2, 14)}[fmt]
    v = np.moveaxis(np.asarray(x, np.float32).astype(ml_dtypes.bfloat16).astype(np.float64), axis, -1)
    blocks = v.reshape(v.shape[:-1] + (-1, 32))
    amax = np.abs(blocks).max(-1, keepdims=True)
    byte = np.maximum(np.where(amax > 0, np.frexp(amax)[1] - 1 + 127, 0) - down, 1)
    scale = np.exp2(byte - 127.0)
    codes = (blocks / scale).astype(np.float32).astype(dtype).astype(np.float64)
    return np.moveaxis((codes * scale).reshape(v.shape), -1, axis)


WIDE = False


def mx_kscale(k):
    if not WIDE:
        return np.ones(k)
    levels = np.array([24, -24, 12, -12, 0])
    if k % 512:
        return np.exp2(np.random.permutation(np.resize(levels, k // 32))).repeat(32)
    a = np.empty((k // 512, 16))
    for p in range(k // 512):
        a[p, :8] = np.random.permutation(np.resize(levels, 8))
        for g in range(8):
            far = levels[np.abs(levels - a[p, g]) >= 10]
            a[p, g + 8] = far[np.random.randint(len(far))]
    return np.exp2(a.ravel()).repeat(32)


def f64(x):
    return np.asarray(x).astype(np.float64)


def striped8(idx):
    return np.concatenate([v.reshape(-1, 16).T for v in idx]).astype(np.uint16)


def unstriped8(offs):
    return np.stack([offs[16 * g:16 * g + 16].T.reshape(-1) for g in range(8)]).astype(np.int64)


E2M1 = np.array([0.0, 0.5, 1.0, 1.5, 2.0, 3.0, 4.0, 6.0, -0.0, -0.5, -1.0, -1.5, -2.0, -3.0, -4.0, -6.0])


def pack_weight(w, fmt):
    k, n = w.shape
    w = f64(np.asarray(w, np.float32).astype(ml_dtypes.bfloat16)).reshape(k // 32, 32, n)
    amax = np.abs(w).max(1)
    if fmt == "e4m3":
        byte = np.frexp(amax)[1] - 1 + 127 - 7
    else:
        mant, ex = np.frexp(amax / 6.0)
        byte = np.where(mant > 0.5, ex, ex - 1) + 127
    byte = np.clip(np.where(amax > 0, byte, 1), 1, 254)
    scaled = (w * np.exp2(127.0 - byte)[:, None, :]).reshape(k, n).astype(np.float32)
    by_word = np.ascontiguousarray(scaled.reshape(k // 512, 128, 4, n).transpose(0, 1, 3, 2))
    if fmt == "e4m3":
        words = by_word.astype(ml_dtypes.float8_e4m3fn).view(np.uint8)
    else:
        c = by_word.astype(ml_dtypes.float4_e2m1fn).view(np.uint8) & 0xF
        words = (c[..., 0::2] | (c[..., 1::2] << 4)).reshape(k // 512, 128, 2 * n)
    return np.ascontiguousarray(words), np.ascontiguousarray(byte.astype(np.uint8).reshape(k // 512, 16, n))


def unpack_weight(words, scales, fmt):
    g, _, n = scales.shape
    words = np.ascontiguousarray(words).reshape(g, 128, n, -1)
    if fmt == "e4m3":
        vals = words.view(ml_dtypes.float8_e4m3fn).astype(np.float64)
    else:
        nib = np.empty((g, 128, n, 4), np.uint8)
        nib[..., 0::2] = words & 0xF
        nib[..., 1::2] = words >> 4
        vals = E2M1[nib]
    vals = vals * np.repeat(np.exp2(scales.astype(np.float64) - 127.0), 8, axis=1)[..., None]
    return vals.transpose(0, 1, 3, 2).reshape(g * 512, n)


def planes(y):
    n, m = y.shape
    v = y.astype(np.float32).astype(ml_dtypes.bfloat16).astype(np.float64).reshape(n // 32, 32, m)
    top = np.abs(v).max(1)
    byte = np.clip(np.where(top > 0, np.frexp(top)[1] - 1 + 127 - 7, 1), 1, 254)
    codes = (v * np.exp2(127.0 - byte)[:, None, :]).reshape(n, m).astype(np.float32).astype(ml_dtypes.float8_e4m3fn).view(np.uint8)
    words = codes.reshape(n // 512, 128, 4, m).transpose(0, 1, 3, 2)
    return np.ascontiguousarray(words), np.ascontiguousarray(byte.astype(np.uint8).reshape(n // 512, 16, m))


def sigm(f):
    return 1.0 / (1.0 + np.exp(-np.maximum(f, -700.0)))


K, N, T, J = 1024, 512, 2048, 1024


def setup_inputs():
    n = np.random.standard_normal
    s = mx_kscale(K)[:, None]
    p_wv = pack_weight(n((K, N)) / np.sqrt(K) / s, "e2m1")
    return {
        "xT": (n((K, T)) * s).astype(np.float32),
        "wgt": np.repeat(np.random.uniform(0.5, 2.0, (8, J)), 16, axis=0).astype(np.float32),
        "wk": (n((K, N)) / np.sqrt(K) / s).astype(np.float32),
        "wv_words": p_wv[0],
        "wv_scales": p_wv[1],
        "bg": (0.3 * n(N) - 1.0).astype(np.float32),
        "res": (n((N, J))).astype(np.float32),
        "offs": striped8(np.stack([np.random.permutation(T)[:J] for _ in range(8)])),
    }


def reference(xT, wgt, wk, wv_words, wv_scales, bg, res, offs):
    idx = unstriped8(offs)
    rows = np.arange(K)
    xg = f64(wgt)[rows // 4 % 128] * f64(xT)[rows[:, None], idx[rows % 512 // 64]]
    xT_ = mxq(xg, 0, "e4m3")
    wk_ = mxq(f64(wk), 0, "e4m3")
    wv_ = unpack_weight(wv_words, wv_scales, "e2m1")
    ke = wk_.T @ xT_
    ve = wv_.T @ xT_
    gate = sigm(ke + f64(bg)[:, None])
    out_0 = f64(res) + gate * (np.tanh(ve) - f64(res))
    return (out_0,) + planes(out_0)

@@ -1,0 +1,282 @@
+from contextlib import ExitStack
+
+import concourse.mybir as mybir
+
+K, N, T, J = 1024, 512, 2048, 1024
+FLOPS = 2 * 2 * K * N * J
+
+F32 = mybir.dt.float32
+BF16 = mybir.dt.bfloat16
+I32 = mybir.dt.int32
+U32 = mybir.dt.uint32
+U16 = mybir.dt.uint16
+U8 = mybir.dt.uint8
+FP8X4 = mybir.dt.float8_e4m3fn_x4
+FP4X4 = mybir.dt.float4_e2m1fn_x4
+ALU = mybir.AluOpType
+TANH = mybir.ActivationFunctionType.Tanh
+
+P = 128
+PACK = 4
+K_PASS = P * PACK
+PASSES = K // K_PASS
+CHUNK = 256
+CHUNKS = J // CHUNK
+LIST = 16
+
+
+def tile_list_hwaytanhP_kernel(
+    tc, xT, wgt, wk, wv_words, wv_scales, bg, res, offs, out_0, out_1, out_2
+):
+    nc = tc.nc
+    with ExitStack() as ctx:
+        keep = ctx.enter_context(tc.tile_pool(name="keep", bufs=1))
+        work = ctx.enter_context(tc.tile_pool(name="work", bufs=2))
+        psum = ctx.enter_context(tc.psum_pool(name="psum", bufs=2))
+
+        def held(name, shape, dtype):
+            return keep.tile(shape, dtype, name=name, align_bytes=64)
+
+        offsets = held("offsets", [P, J // LIST], U16)
+        wv_raw = held("wv_raw", [P, PASSES, 2 * N], U8)
+        wvs_raw = held("wvs_raw", [P, PASSES, N], U8)
+        wv_codes = held("wv_codes", [P, PASSES, 2 * N], U8)
+        wv_scale = held("wv_scale", [P, PASSES, N], U8)
+        weights = held("weights", [P, J], F32)
+        bias = held("bias", [P, PACK], F32)
+        half_bias = held("half_bias", [P, PACK], F32)
+        planes = [[held("x%d%d" % (a, i), [P, T], F32) for i in range(PACK)] for a in range(PASSES)]
+        picked = [held("picked%d" % a, [P, PACK, J], F32) for a in range(PASSES)]
+        xg_codes = [held("xg_codes%d" % a, [P, J], U32) for a in range(PASSES)]
+        xg_scale = [held("xg_scale%d" % a, [P, J], U8) for a in range(PASSES)]
+        wk_raw = [[held("wk_raw%d%d" % (a, h), [P, PACK, N // 2], F32) for h in range(2)] for a in range(PASSES)]
+        wk_bf = [held("wk_bf%d" % a, [P, PACK, P, PACK], BF16) for a in range(PASSES)]
+        wk_codes = [held("wk_codes%d" % a, [P, N], U32) for a in range(PASSES)]
+        wk_scale = [held("wk_scale%d" % a, [P, N], U8) for a in range(PASSES)]
+        carried = [held("carried%d" % c, [P, PACK, CHUNK], F32) for c in range(CHUNKS)]
+        out_scale = held("out_scale", [P, J], U8)
+        warm = held("warm", [P, 8], F32)
+
+        def load_plane(a, i):
+            rows = xT[a * K_PASS : (a + 1) * K_PASS, :].rearrange("(p i) t -> p i t", i=PACK)
+            nc.sync.dma_start(out=planes[a][i][:], in_=rows[:, i, :])
+
+        def load_wk(a, h):
+            rows = wk[a * K_PASS : (a + 1) * K_PASS, :].rearrange("(p i) n -> p i n", i=PACK)
+            nc.sync.dma_start(out=wk_raw[a][h][:], in_=rows[:, :, h * (N // 2) : (h + 1) * (N // 2)])
+
+        def gather(a, i, j0, j1):
+            nc.vector.tensor_tensor(
+                picked[a][:, i, j0:j1],
+                planes[a][i][:].indirect(offsets[:, j0 // LIST : j1 // LIST]),
+                weights[:, j0:j1],
+                ALU.mult,
+            )
+
+        def copy_on(engine, out, in_):
+            if engine == "vector":
+                nc.vector.tensor_copy(out=out, in_=in_)
+            else:
+                nc.scalar.copy(out=out, in_=in_)
+
+        def interleave(engine, src, width, tag, bufs):
+            dst = work.tile([P, width * PACK], BF16, name=tag, align_bytes=64, bufs=bufs)
+            copy_on(
+                engine,
+                dst[:].rearrange("p (c e i) -> p c i e", e=4, i=PACK),
+                src.rearrange("p i (c e) -> p c i e", e=4),
+            )
+            return dst
+
+        def quantize_xg(a, src, j0, j1):
+            nc.vector.quantize_mx(out=xg_codes[a][:, j0:j1].bitcast(FP8X4), scales=xg_scale[a][:, j0:j1], in_=src[:])
+
+        def deal_wk(engine, a, h):
+            copy_on(
+                engine,
+                wk_bf[a][:, :, h * (P // 2) : (h + 1) * (P // 2), :].rearrange("p t m i -> p m i t"),
+                wk_raw[a][h][:].rearrange("p i (m t) -> p m i t", t=PACK),
+            )
+
+        def quantize_wk(a):
+            nc.vector.quantize_mx(
+                out=wk_codes[a][:].bitcast(FP8X4),
+                scales=wk_scale[a][:],
+                in_=wk_bf[a][:].rearrange("p t m i -> p (t m i)"),
+            )
+
+        def new_banks(kind):
+            return [psum.tile([P, 2, CHUNK], F32, name="%s%d" % (kind, u)) for u in range(2)]
+
+        def value_pass(banks, c, a):
+            for t in range(PACK):
+                for s in range(CHUNK // P):
+                    cols = slice(c * CHUNK + s * P, c * CHUNK + (s + 1) * P)
+                    nc.tensor.matmul_mx(
+                        out=banks[t // 2][:, t % 2, s * P : (s + 1) * P],
+                        lhsT=wv_codes[:, a, 2 * P * t : 2 * P * (t + 1)].bitcast(FP4X4),
+                        lhsT_scale=wv_scale[:, a, P * t : P * (t + 1)],
+                        rhs=xg_codes[a][:, cols].bitcast(FP8X4),
+                        rhs_scale=xg_scale[a][:, cols],
+                        start=(a == 0 and t % 2 == 0 and s == 0),
+                        stop=(a == PASSES - 1 and t % 2 == 1 and s == CHUNK // P - 1),
+                    )
+
+        def key_pass(banks, c, a):
+            cols = slice(c * CHUNK, (c + 1) * CHUNK)
+            for t in range(PACK):
+                nc.tensor.matmul_mx(
+                    out=banks[t // 2][:, t % 2, :],
+                    lhsT=wk_codes[a][:, P * t : P * (t + 1)].bitcast(FP8X4),
+                    lhsT_scale=wk_scale[a][:, P * t : P * (t + 1)],
+                    rhs=xg_codes[a][:, cols].bitcast(FP8X4),
+                    rhs_scale=xg_scale[a][:, cols],
+                    start=(a == 0 and t % 2 == 0),
+                    stop=(a == PASSES - 1 and t % 2 == 1),
+                )
+
+        def value_tanh(banks):
+            tv = work.tile([P, PACK, CHUNK], F32, name="tv")
+            for u in range(2):
+                nc.scalar.activation(out=tv[:, 2 * u : 2 * u + 2, :], in_=banks[u][:], func=TANH)
+            return tv
+
+        def key_tanh(banks):
+            th = work.tile([P, PACK, CHUNK], F32, name="th")
+            for t in range(PACK):
+                nc.scalar.activation(
+                    out=th[:, t, :], in_=banks[t // 2][:, t % 2, :], func=TANH, bias=half_bias[:, t : t + 1], scale=0.5
+                )
+            return th
+
+        def difference(c, tv):
+            diff = work.tile([P, PACK, CHUNK], F32, name="diff", bufs=1)
+            nc.vector.tensor_tensor(diff[:], tv[:], carried[c][:], ALU.subtract)
+            return diff
+
+        def gated(th, diff):
+            twice = work.tile([P, PACK, CHUNK], F32, name="twice")
+            nc.vector.scalar_tensor_tensor(twice[:], th[:], 1.0, diff[:], ALU.add, ALU.mult)
+            return twice
+
+        def finish(c, twice):
+            y = work.tile([P, PACK, CHUNK], F32, name="y", bufs=3)
+            nc.vector.scalar_tensor_tensor(y[:], twice[:], 0.5, carried[c][:], ALU.mult, ALU.add)
+            rows = out_0.rearrange("(p t) j -> p t j", t=PACK)
+            nc.sync.dma_start(out=rows[:, :, c * CHUNK : (c + 1) * CHUNK], in_=y[:])
+            return y
+
+        def quantize_out(c, src):
+            codes = work.tile([P, CHUNK], U32, name="out_codes", align_bytes=64, bufs=4)
+            cols = slice(c * CHUNK, (c + 1) * CHUNK)
+            nc.vector.quantize_mx(out=codes[:].bitcast(FP8X4), scales=out_scale[:, cols], in_=src[:])
+            words = out_1[0].rearrange("p j t -> p (j t)").bitcast(I32)
+            nc.sync.dma_start(out=words[:, cols], in_=codes[:].bitcast(I32))
+
+        nc.vector.memset(wvs_raw[:].rearrange("p a n -> p (a n)").bitcast(I32), 0)
+        nc.vector.memset(warm[:], 0.0)
+        nc.sync.dma_start(offsets[:], offs)
+        nc.sync.dma_start(out=wv_raw[:].bitcast(I32), in_=wv_words.rearrange("a p b -> p a b").bitcast(I32))
+        nc.sync.dma_start(out=weights[:, : J // 2], in_=wgt[:, : J // 2])
+        load_plane(0, 0)
+        for q in range(4):
+            nc.scalar.dma_start(
+                out=wvs_raw[32 * q : 32 * q + 4, :, :].bitcast(I32),
+                in_=wv_scales[:, 4 * q : 4 * q + 4, :].rearrange("a r n -> r a n").bitcast(I32),
+            )
+        nc.scalar.activation(out=warm[:, 4:5], in_=warm[:, 0:1], func=TANH)
+        nc.sync.dma_start(out=weights[:, J // 2 :], in_=wgt[:, J // 2 :])
+        for i in range(1, PACK):
+            load_plane(0, i)
+        nc.sync.dma_start(out=bias[:], in_=bg.rearrange("(p t) -> p t", t=PACK))
+        load_plane(1, 0)
+        load_wk(0, 0)
+        load_wk(0, 1)
+        for i in range(1, PACK):
+            load_plane(1, i)
+        load_wk(1, 0)
+        load_wk(1, 1)
+        res_rows = res.rearrange("(p t) j -> p t j", t=PACK)
+        for c in range(CHUNKS):
+            nc.sync.dma_start(out=carried[c][:], in_=res_rows[:, :, c * CHUNK : (c + 1) * CHUNK])
+
+        nc.vector.tensor_copy(
+            out=wv_codes[:].rearrange("p a (t m b) -> p a t m b", t=PACK, b=2),
+            in_=wv_raw[:].rearrange("p a (m t b) -> p a t m b", t=PACK, b=2),
+        )
+        nc.vector.tensor_copy(
+            out=wv_scale[:].rearrange("p a (t m) -> p a t m", t=PACK),
+            in_=wvs_raw[:].rearrange("p a (m t) -> p a t m", t=PACK),
+        )
+
+        gather(0, 0, 0, J // 2)
+        gather(0, 0, J // 2, J)
+        for i in range(1, PACK):
+            gather(0, i, 0, J)
+        nc.vector.tensor_scalar(half_bias[:], bias[:], 0.5, None, ALU.mult)
+        first = [interleave("scalar", picked[0][:, :, h * 512 : (h + 1) * 512], 512, "xb0", 2) for h in range(2)]
+        gather(1, 0, 0, J)
+        quantize_xg(0, first[0], 0, 512)
+        deal_wk("scalar", 0, 0)
+        deal_wk("scalar", 0, 1)
+        quantize_xg(0, first[1], 512, J)
+        gather(1, 1, 0, J)
+        quantize_wk(0)
+        gather(1, 2, 0, J)
+
+        vb = {}
+        kb = {}
+        for c in range(2):
+            vb[c] = new_banks("ve")
+            kb[c] = new_banks("ke")
+            value_pass(vb[c], c, 0)
+            key_pass(kb[c], c, 0)
+
+        def xg_chunk(engine, c):
+            return interleave(engine, picked[1][:, :, c * CHUNK : (c + 1) * CHUNK], CHUNK, "xb1", 4)
+
+        gather(1, 3, 0, CHUNK)
+        xb = {0: xg_chunk("scalar", 0)}
+        deal_wk("scalar", 1, 0)
+        for c in range(1, CHUNKS):
+            gather(1, 3, c * CHUNK, (c + 1) * CHUNK)
+        quantize_xg(1, xb[0], 0, CHUNK)
+        value_pass(vb[0], 0, 1)
+        deal_wk("vector", 1, 1)
+        xb[1] = xg_chunk("vector", 1)
+        quantize_wk(1)
+        key_pass(kb[0], 0, 1)
+        quantize_xg(1, xb[1], CHUNK, 2 * CHUNK)
+        value_pass(vb[1], 1, 1)
+        key_pass(kb[1], 1, 1)
+
+        yb = {}
+        y = {}
+        for c in range(CHUNKS):
+            tv = value_tanh(vb[c])
+            th = key_tanh(kb[c])
+            nxt = c + 2
+            if nxt < CHUNKS:
+                xb[nxt] = xg_chunk("scalar", nxt)
+                vb[nxt] = new_banks("ve")
+                kb[nxt] = new_banks("ke")
+                value_pass(vb[nxt], nxt, 0)
+                key_pass(kb[nxt], nxt, 0)
+            if c > 0:
+                yb[c - 1] = interleave("scalar", y[c - 1][:], CHUNK, "yb", 2)
+            diff = difference(c, tv)
+            twice = gated(th, diff)
+            if nxt < CHUNKS:
+                quantize_xg(1, xb[nxt], nxt * CHUNK, (nxt + 1) * CHUNK)
+                value_pass(vb[nxt], nxt, 1)
+                key_pass(kb[nxt], nxt, 1)
+            y[c] = finish(c, twice)
+            if c > 0:
+                quantize_out(c - 1, yb[c - 1])
+        last = CHUNKS - 1
+        quantize_out(last, interleave("vector", y[last][:], CHUNK, "yb", 2))
+        for q in range(4):
+            eng = nc.sync if q % 2 == 0 else nc.scalar
+            eng.dma_start(
+                out=out_2[0, 4 * q : 4 * q + 4, :].bitcast(I32), in_=out_scale[32 * q : 32 * q + 4, :].bitcast(I32)
+            )

@@ -20,8 +20,10 @@ P = 128
 PACK = 4
 K_PASS = P * PACK
 PASSES = K // K_PASS
-CHUNK = 256
-CHUNKS = J // CHUNK
+WIDTHS = [128, 256, 256, 256, 128]
+STARTS = [sum(WIDTHS[:c]) for c in range(len(WIDTHS))]
+CHUNKS = len(WIDTHS)
+BANK = 512
 LIST = 16
 
 
@@ -32,7 +34,7 @@ def tile_list_hwaytanhP_kernel(
     with ExitStack() as ctx:
         keep = ctx.enter_context(tc.tile_pool(name="keep", bufs=1))
         work = ctx.enter_context(tc.tile_pool(name="work", bufs=2))
-        psum = ctx.enter_context(tc.psum_pool(name="psum", bufs=2))
+        psum = ctx.enter_context(tc.psum_pool(name="psum", bufs=8))
 
         def held(name, shape, dtype):
             return keep.tile(shape, dtype, name=name, align_bytes=64)
@@ -45,15 +47,15 @@ def tile_list_hwaytanhP_kernel(
         weights = held("weights", [P, J], F32)
         bias = held("bias", [P, PACK], F32)
         half_bias = held("half_bias", [P, PACK], F32)
-        planes = [[held("x%d%d" % (a, i), [P, T], F32) for i in range(PACK)] for a in range(PASSES)]
-        picked = [held("picked%d" % a, [P, PACK, J], F32) for a in range(PASSES)]
+        planes = [[work.tile([P, T], F32, name="x", bufs=6) for i in range(PACK)] for a in range(PASSES)]
+        picked = [held("picked%d" % a, [P, PACK * J], F32) for a in range(PASSES)]
         xg_codes = [held("xg_codes%d" % a, [P, J], U32) for a in range(PASSES)]
         xg_scale = [held("xg_scale%d" % a, [P, J], U8) for a in range(PASSES)]
         wk_raw = [[held("wk_raw%d%d" % (a, h), [P, PACK, N // 2], F32) for h in range(2)] for a in range(PASSES)]
         wk_bf = [held("wk_bf%d" % a, [P, PACK, P, PACK], BF16) for a in range(PASSES)]
         wk_codes = [held("wk_codes%d" % a, [P, N], U32) for a in range(PASSES)]
         wk_scale = [held("wk_scale%d" % a, [P, N], U8) for a in range(PASSES)]
-        carried = [held("carried%d" % c, [P, PACK, CHUNK], F32) for c in range(CHUNKS)]
+        carried = [held("carried%d" % c, [P, PACK, WIDTHS[c]], F32) for c in range(CHUNKS)]
         out_scale = held("out_scale", [P, J], U8)
         warm = held("warm", [P, 8], F32)
 
@@ -65,9 +67,12 @@ def tile_list_hwaytanhP_kernel(
             rows = wk[a * K_PASS : (a + 1) * K_PASS, :].rearrange("(p i) n -> p i n", i=PACK)
             nc.sync.dma_start(out=wk_raw[a][h][:], in_=rows[:, :, h * (N // 2) : (h + 1) * (N // 2)])
 
+        def rows_of(a):
+            return picked[a][:].rearrange("p (i j) -> p i j", i=PACK)
+
         def gather(a, i, j0, j1):
             nc.vector.tensor_tensor(
-                picked[a][:, i, j0:j1],
+                picked[a][:, i * J + j0 : i * J + j1],
                 planes[a][i][:].indirect(offsets[:, j0 // LIST : j1 // LIST]),
                 weights[:, j0:j1],
                 ALU.mult,
@@ -105,176 +110,230 @@ def tile_list_hwaytanhP_kernel(
                 in_=wk_bf[a][:].rearrange("p t m i -> p (t m i)"),
             )
 
-        def new_banks(kind):
-            return [psum.tile([P, 2, CHUNK], F32, name="%s%d" % (kind, u)) for u in range(2)]
+        def cols_of(c):
+            return slice(STARTS[c], STARTS[c] + WIDTHS[c])
+
+        def new_banks(c):
+            count = PACK * WIDTHS[c] // BANK
+            return [psum.tile([P, BANK], F32, name="bank") for u in range(count)]
+
+        def place(banks, c, t):
+            per_bank = BANK // WIDTHS[c]
+            lo = (t % per_bank) * WIDTHS[c]
+            return banks[t // per_bank], lo, t % per_bank == 0, t % per_bank == per_bank - 1
 
         def value_pass(banks, c, a):
+            pieces = WIDTHS[c] // P
             for t in range(PACK):
-                for s in range(CHUNK // P):
-                    cols = slice(c * CHUNK + s * P, c * CHUNK + (s + 1) * P)
+                bank, lo, opens, closes = place(banks, c, t)
+                for s in range(pieces):
+                    cols = slice(STARTS[c] + s * P, STARTS[c] + (s + 1) * P)
                     nc.tensor.matmul_mx(
-                        out=banks[t // 2][:, t % 2, s * P : (s + 1) * P],
+                        out=bank[:, lo + s * P : lo + (s + 1) * P],
                         lhsT=wv_codes[:, a, 2 * P * t : 2 * P * (t + 1)].bitcast(FP4X4),
                         lhsT_scale=wv_scale[:, a, P * t : P * (t + 1)],
                         rhs=xg_codes[a][:, cols].bitcast(FP8X4),
                         rhs_scale=xg_scale[a][:, cols],
-                        start=(a == 0 and t % 2 == 0 and s == 0),
-                        stop=(a == PASSES - 1 and t % 2 == 1 and s == CHUNK // P - 1),
+                        start=(a == 0 and opens and s == 0),
+                        stop=(a == PASSES - 1 and closes and s == pieces - 1),
                     )
 
         def key_pass(banks, c, a):
-            cols = slice(c * CHUNK, (c + 1) * CHUNK)
+            cols = cols_of(c)
             for t in range(PACK):
+                bank, lo, opens, closes = place(banks, c, t)
                 nc.tensor.matmul_mx(
-                    out=banks[t // 2][:, t % 2, :],
+                    out=bank[:, lo : lo + WIDTHS[c]],
                     lhsT=wk_codes[a][:, P * t : P * (t + 1)].bitcast(FP8X4),
                     lhsT_scale=wk_scale[a][:, P * t : P * (t + 1)],
                     rhs=xg_codes[a][:, cols].bitcast(FP8X4),
                     rhs_scale=xg_scale[a][:, cols],
-                    start=(a == 0 and t % 2 == 0),
-                    stop=(a == PASSES - 1 and t % 2 == 1),
+                    start=(a == 0 and opens),
+                    stop=(a == PASSES - 1 and closes),
                 )
 
-        def value_tanh(banks):
-            tv = work.tile([P, PACK, CHUNK], F32, name="tv")
-            for u in range(2):
-                nc.scalar.activation(out=tv[:, 2 * u : 2 * u + 2, :], in_=banks[u][:], func=TANH)
+        def value_tanh(banks, c):
+            tv = work.tile([P, PACK * WIDTHS[c]], F32, name="tv", bufs=3)
+            for u, bank in enumerate(banks):
+                nc.scalar.activation(out=tv[:, u * BANK : (u + 1) * BANK], in_=bank[:], func=TANH)
             return tv
 
-        def key_tanh(banks):
-            th = work.tile([P, PACK, CHUNK], F32, name="th")
+        def key_tanh(banks, c):
+            w = WIDTHS[c]
+            th = work.tile([P, PACK * w], F32, name="th")
             for t in range(PACK):
+                bank, lo, opens, closes = place(banks, c, t)
                 nc.scalar.activation(
-                    out=th[:, t, :], in_=banks[t // 2][:, t % 2, :], func=TANH, bias=half_bias[:, t : t + 1], scale=0.5
+                    out=th[:, t * w : (t + 1) * w],
+                    in_=bank[:, lo : lo + w],
+                    func=TANH,
+                    bias=half_bias[:, t : t + 1],
+                    scale=0.5,
                 )
             return th
 
+        def flat(tile):
+            return tile[:].rearrange("p t j -> p (t j)")
+
         def difference(c, tv):
-            diff = work.tile([P, PACK, CHUNK], F32, name="diff", bufs=1)
-            nc.vector.tensor_tensor(diff[:], tv[:], carried[c][:], ALU.subtract)
+            diff = work.tile([P, PACK * WIDTHS[c]], F32, name="diff")
+            nc.vector.tensor_tensor(diff[:], tv[:], flat(carried[c]), ALU.subtract)
             return diff
 
-        def gated(th, diff):
-            twice = work.tile([P, PACK, CHUNK], F32, name="twice")
+        def gated(c, th, diff):
+            twice = work.tile([P, PACK * WIDTHS[c]], F32, name="twice")
             nc.vector.scalar_tensor_tensor(twice[:], th[:], 1.0, diff[:], ALU.add, ALU.mult)
             return twice
 
         def finish(c, twice):
-            y = work.tile([P, PACK, CHUNK], F32, name="y", bufs=3)
-            nc.vector.scalar_tensor_tensor(y[:], twice[:], 0.5, carried[c][:], ALU.mult, ALU.add)
+            y = work.tile([P, PACK, WIDTHS[c]], F32, name="y", bufs=4)
+            nc.vector.scalar_tensor_tensor(flat(y), twice[:], 0.5, flat(carried[c]), ALU.mult, ALU.add)
             rows = out_0.rearrange("(p t) j -> p t j", t=PACK)
-            nc.sync.dma_start(out=rows[:, :, c * CHUNK : (c + 1) * CHUNK], in_=y[:])
+            nc.sync.dma_start(out=rows[:, :, cols_of(c)], in_=y[:])
             return y
 
         def quantize_out(c, src):
-            codes = work.tile([P, CHUNK], U32, name="out_codes", align_bytes=64, bufs=4)
-            cols = slice(c * CHUNK, (c + 1) * CHUNK)
-            nc.vector.quantize_mx(out=codes[:].bitcast(FP8X4), scales=out_scale[:, cols], in_=src[:])
+            codes = work.tile([P, WIDTHS[c]], U32, name="out_codes", align_bytes=64, bufs=4)
+            nc.vector.quantize_mx(out=codes[:].bitcast(FP8X4), scales=out_scale[:, cols_of(c)], in_=src[:])
             words = out_1[0].rearrange("p j t -> p (j t)").bitcast(I32)
-            nc.sync.dma_start(out=words[:, cols], in_=codes[:].bitcast(I32))
+            nc.sync.dma_start(out=words[:, cols_of(c)], in_=codes[:].bitcast(I32))
 
+        def load_res(c):
+            res_rows = res.rearrange("(p t) j -> p t j", t=PACK)
+            nc.sync.dma_start(out=carried[c][:], in_=res_rows[:, :, cols_of(c)])
+
+
+        FIRST = 256
         nc.vector.memset(wvs_raw[:].rearrange("p a n -> p (a n)").bitcast(I32), 0)
         nc.vector.memset(warm[:], 0.0)
         nc.sync.dma_start(offsets[:], offs)
         nc.sync.dma_start(out=wv_raw[:].bitcast(I32), in_=wv_words.rearrange("a p b -> p a b").bitcast(I32))
-        nc.sync.dma_start(out=weights[:, : J // 2], in_=wgt[:, : J // 2])
+        nc.sync.dma_start(out=weights[:, :FIRST], in_=wgt[:, :FIRST])
         load_plane(0, 0)
+        nc.sync.dma_start(out=weights[:, FIRST:], in_=wgt[:, FIRST:])
         for q in range(4):
             nc.scalar.dma_start(
                 out=wvs_raw[32 * q : 32 * q + 4, :, :].bitcast(I32),
                 in_=wv_scales[:, 4 * q : 4 * q + 4, :].rearrange("a r n -> r a n").bitcast(I32),
             )
         nc.scalar.activation(out=warm[:, 4:5], in_=warm[:, 0:1], func=TANH)
-        nc.sync.dma_start(out=weights[:, J // 2 :], in_=wgt[:, J // 2 :])
-        for i in range(1, PACK):
-            load_plane(0, i)
+        load_plane(0, 1)
+        load_plane(0, 2)
+        load_plane(0, 3)
         nc.sync.dma_start(out=bias[:], in_=bg.rearrange("(p t) -> p t", t=PACK))
         load_plane(1, 0)
+        load_plane(1, 1)
         load_wk(0, 0)
+        load_plane(1, 2)
         load_wk(0, 1)
-        for i in range(1, PACK):
-            load_plane(1, i)
+        load_plane(1, 3)
         load_wk(1, 0)
         load_wk(1, 1)
-        res_rows = res.rearrange("(p t) j -> p t j", t=PACK)
         for c in range(CHUNKS):
-            nc.sync.dma_start(out=carried[c][:], in_=res_rows[:, :, c * CHUNK : (c + 1) * CHUNK])
+            load_res(c)
 
         nc.vector.tensor_copy(
-            out=wv_codes[:].rearrange("p a (t m b) -> p a t m b", t=PACK, b=2),
-            in_=wv_raw[:].rearrange("p a (m t b) -> p a t m b", t=PACK, b=2),
+            out=wv_codes[:].bitcast(U16).rearrange("p a (t m) -> p a t m", t=PACK),
+            in_=wv_raw[:].bitcast(U16).rearrange("p a (m t) -> p a t m", t=PACK),
         )
+        gather(0, 0, 0, FIRST)
+        gather(0, 0, FIRST, J)
         nc.vector.tensor_copy(
             out=wv_scale[:].rearrange("p a (t m) -> p a t m", t=PACK),
             in_=wvs_raw[:].rearrange("p a (m t) -> p a t m", t=PACK),
         )
-
-        gather(0, 0, 0, J // 2)
-        gather(0, 0, J // 2, J)
         for i in range(1, PACK):
             gather(0, i, 0, J)
+        first = [interleave("scalar", rows_of(0)[:, :, h * 512 : (h + 1) * 512], 512, "xb0", 2) for h in range(2)]
         nc.vector.tensor_scalar(half_bias[:], bias[:], 0.5, None, ALU.mult)
-        first = [interleave("scalar", picked[0][:, :, h * 512 : (h + 1) * 512], 512, "xb0", 2) for h in range(2)]
         gather(1, 0, 0, J)
         quantize_xg(0, first[0], 0, 512)
+        gather(1, 1, 0, J)
+        quantize_xg(0, first[1], 512, J)
         deal_wk("scalar", 0, 0)
         deal_wk("scalar", 0, 1)
-        quantize_xg(0, first[1], 512, J)
-        gather(1, 1, 0, J)
-        quantize_wk(0)
         gather(1, 2, 0, J)
+        quantize_wk(0)
 
         vb = {}
         kb = {}
-        for c in range(2):
-            vb[c] = new_banks("ve")
-            kb[c] = new_banks("ke")
+        xb = {}
+
+        def open_chunk(c):
+            vb[c] = new_banks(c)
+            kb[c] = new_banks(c)
             value_pass(vb[c], c, 0)
             key_pass(kb[c], c, 0)
 
         def xg_chunk(engine, c):
-            return interleave(engine, picked[1][:, :, c * CHUNK : (c + 1) * CHUNK], CHUNK, "xb1", 4)
+            xb[c] = interleave(engine, rows_of(1)[:, :, cols_of(c)], WIDTHS[c], "xb1", 4)
 
-        gather(1, 3, 0, CHUNK)
-        xb = {0: xg_chunk("scalar", 0)}
+        def close_value(c):
+            quantize_xg(1, xb[c], STARTS[c], STARTS[c] + WIDTHS[c])
+            value_pass(vb[c], c, 1)
+
+        def close_chunk(c):
+            close_value(c)
+            key_pass(kb[c], c, 1)
+
+        def last_plane(c):
+            gather(1, 3, STARTS[c], STARTS[c] + WIDTHS[c])
+
+        open_chunk(0)
+        open_chunk(1)
         deal_wk("scalar", 1, 0)
-        for c in range(1, CHUNKS):
-            gather(1, 3, c * CHUNK, (c + 1) * CHUNK)
-        quantize_xg(1, xb[0], 0, CHUNK)
-        value_pass(vb[0], 0, 1)
+        last_plane(0)
+        last_plane(1)
+        xg_chunk("vector", 0)
+        xg_chunk("vector", 1)
+        close_value(0)
+        close_value(1)
         deal_wk("vector", 1, 1)
-        xb[1] = xg_chunk("vector", 1)
+        last_plane(2)
         quantize_wk(1)
         key_pass(kb[0], 0, 1)
-        quantize_xg(1, xb[1], CHUNK, 2 * CHUNK)
-        value_pass(vb[1], 1, 1)
         key_pass(kb[1], 1, 1)
+        gather(1, 3, STARTS[3], J)
 
-        yb = {}
+        tv = {}
+
+        def values(c):
+            vb[c] = new_banks(c)
+            value_pass(vb[c], c, 0)
+            close_value(c)
+            tv[c] = value_tanh(vb[c], c)
+
+        def keys(c):
+            kb[c] = new_banks(c)
+            key_pass(kb[c], c, 0)
+            key_pass(kb[c], c, 1)
+
+        xg_chunk("scalar", 2)
+        for c in range(2):
+            tv[c] = value_tanh(vb[c], c)
+        diff = {0: difference(0, tv[0])}
+        values(2)
         y = {}
         for c in range(CHUNKS):
-            tv = value_tanh(vb[c])
-            th = key_tanh(kb[c])
-            nxt = c + 2
-            if nxt < CHUNKS:
-                xb[nxt] = xg_chunk("scalar", nxt)
-                vb[nxt] = new_banks("ve")
-                kb[nxt] = new_banks("ke")
-                value_pass(vb[nxt], nxt, 0)
-                key_pass(kb[nxt], nxt, 0)
-            if c > 0:
-                yb[c - 1] = interleave("scalar", y[c - 1][:], CHUNK, "yb", 2)
-            diff = difference(c, tv)
-            twice = gated(th, diff)
-            if nxt < CHUNKS:
-                quantize_xg(1, xb[nxt], nxt * CHUNK, (nxt + 1) * CHUNK)
-                value_pass(vb[nxt], nxt, 1)
-                key_pass(kb[nxt], nxt, 1)
+            th = key_tanh(kb[c], c)
+            if c + 3 < CHUNKS:
+                xg_chunk("scalar", c + 3)
+            if c + 2 < CHUNKS:
+                keys(c + 2)
+            if c + 1 < CHUNKS:
+                diff[c + 1] = difference(c + 1, tv[c + 1])
+            twice = gated(c, th, diff[c])
+            if c + 3 < CHUNKS:
+                values(c + 3)
             y[c] = finish(c, twice)
-            if c > 0:
-                quantize_out(c - 1, yb[c - 1])
         last = CHUNKS - 1
-        quantize_out(last, interleave("vector", y[last][:], CHUNK, "yb", 2))
+        yb = {c: interleave("scalar", y[c][:], WIDTHS[c], "yb", 4) for c in range(last)}
+        for c in range(last - 1):
+            quantize_out(c, yb[c])
+        tail = interleave("vector", y[last][:], WIDTHS[last], "yb", 4)
+        quantize_out(last - 1, yb[last - 1])
+        quantize_out(last, tail)
+
         for q in range(4):
             eng = nc.sync if q % 2 == 0 else nc.scalar
             eng.dma_start(

@@ -47,15 +47,21 @@ def tile_list_hwaytanhP_kernel(
         weights = held("weights", [P, J], F32)
         bias = held("bias", [P, PACK], F32)
         half_bias = held("half_bias", [P, PACK], F32)
-        planes = [[work.tile([P, T], F32, name="x", bufs=6) for i in range(PACK)] for a in range(PASSES)]
+        planes = [
+            [keep.tile([P, T], F32, name="x", tag="x%d" % ((PACK * a + i) % 6), align_bytes=64) for i in range(PACK)]
+            for a in range(PASSES)
+        ]
         picked = [held("picked%d" % a, [P, PACK * J], F32) for a in range(PASSES)]
-        xg_codes = [held("xg_codes%d" % a, [P, J], U32) for a in range(PASSES)]
+        xg_codes = {1: held("xg_codes1", [P, J], U32)}
+        xb0 = held("xb0", [P, J * PACK], BF16)
+        xb1 = [held("xb1%d" % c, [P, WIDTHS[c] * PACK], BF16) for c in range(CHUNKS)]
         xg_scale = [held("xg_scale%d" % a, [P, J], U8) for a in range(PASSES)]
         wk_raw = [[held("wk_raw%d%d" % (a, h), [P, PACK, N // 2], F32) for h in range(2)] for a in range(PASSES)]
         wk_bf = [held("wk_bf%d" % a, [P, PACK, P, PACK], BF16) for a in range(PASSES)]
-        wk_codes = [held("wk_codes%d" % a, [P, N], U32) for a in range(PASSES)]
+        wk_codes = {1: held("wk_codes1", [P, N], U32)}
         wk_scale = [held("wk_scale%d" % a, [P, N], U8) for a in range(PASSES)]
         carried = [held("carried%d" % c, [P, PACK, WIDTHS[c]], F32) for c in range(CHUNKS)]
+        out_codes = held("out_codes", [P, J], U32)
         out_scale = held("out_scale", [P, J], U8)
         warm = held("warm", [P, 8], F32)
 
@@ -92,6 +98,13 @@ def tile_list_hwaytanhP_kernel(
                 src.rearrange("p i (c e) -> p c i e", e=4),
             )
             return dst
+
+        def weave_pair(engine, dst, a, u, cols):
+            copy_on(
+                engine,
+                dst[:].rearrange("p (c e i) -> p c i e", e=4, i=PACK)[:, :, 2 * u : 2 * u + 2, :],
+                rows_of(a)[:, 2 * u : 2 * u + 2, cols].rearrange("p i (c e) -> p c i e", e=4),
+            )
 
         def quantize_xg(a, src, j0, j1):
             nc.vector.quantize_mx(out=xg_codes[a][:, j0:j1].bitcast(FP8X4), scales=xg_scale[a][:, j0:j1], in_=src[:])
@@ -160,7 +173,7 @@ def tile_list_hwaytanhP_kernel(
 
         def key_tanh(banks, c):
             w = WIDTHS[c]
-            th = work.tile([P, PACK * w], F32, name="th")
+            th = work.tile([P, PACK * w], F32, name="th", bufs=3)
             for t in range(PACK):
                 bank, lo, opens, closes = place(banks, c, t)
                 nc.scalar.activation(
@@ -186,17 +199,18 @@ def tile_list_hwaytanhP_kernel(
             return twice
 
         def finish(c, twice):
-            y = work.tile([P, PACK, WIDTHS[c]], F32, name="y", bufs=4)
+            y = work.tile([P, PACK, WIDTHS[c]], F32, name="y", bufs=3)
             nc.vector.scalar_tensor_tensor(flat(y), twice[:], 0.5, flat(carried[c]), ALU.mult, ALU.add)
             rows = out_0.rearrange("(p t) j -> p t j", t=PACK)
             nc.sync.dma_start(out=rows[:, :, cols_of(c)], in_=y[:])
             return y
 
-        def quantize_out(c, src):
-            codes = work.tile([P, WIDTHS[c]], U32, name="out_codes", align_bytes=64, bufs=4)
-            nc.vector.quantize_mx(out=codes[:].bitcast(FP8X4), scales=out_scale[:, cols_of(c)], in_=src[:])
+        def quantize_out(cols, src):
+            nc.vector.quantize_mx(out=out_codes[:, cols].bitcast(FP8X4), scales=out_scale[:, cols], in_=src[:])
+
+        def store_codes(cols):
             words = out_1[0].rearrange("p j t -> p (j t)").bitcast(I32)
-            nc.sync.dma_start(out=words[:, cols_of(c)], in_=codes[:].bitcast(I32))
+            nc.sync.dma_start(out=words[:, cols], in_=out_codes[:, cols].bitcast(I32))
 
         def load_res(c):
             res_rows = res.rearrange("(p t) j -> p t j", t=PACK)
@@ -209,13 +223,13 @@ def tile_list_hwaytanhP_kernel(
         nc.sync.dma_start(offsets[:], offs)
         nc.sync.dma_start(out=wv_raw[:].bitcast(I32), in_=wv_words.rearrange("a p b -> p a b").bitcast(I32))
         nc.sync.dma_start(out=weights[:, :FIRST], in_=wgt[:, :FIRST])
-        load_plane(0, 0)
-        nc.sync.dma_start(out=weights[:, FIRST:], in_=wgt[:, FIRST:])
         for q in range(4):
-            nc.scalar.dma_start(
+            nc.sync.dma_start(
                 out=wvs_raw[32 * q : 32 * q + 4, :, :].bitcast(I32),
                 in_=wv_scales[:, 4 * q : 4 * q + 4, :].rearrange("a r n -> r a n").bitcast(I32),
             )
+        load_plane(0, 0)
+        nc.sync.dma_start(out=weights[:, FIRST:], in_=wgt[:, FIRST:])
         nc.scalar.activation(out=warm[:, 4:5], in_=warm[:, 0:1], func=TANH)
         load_plane(0, 1)
         load_plane(0, 2)
@@ -224,10 +238,10 @@ def tile_list_hwaytanhP_kernel(
         load_plane(1, 0)
         load_plane(1, 1)
         load_wk(0, 0)
-        load_plane(1, 2)
         load_wk(0, 1)
-        load_plane(1, 3)
+        load_plane(1, 2)
         load_wk(1, 0)
+        load_plane(1, 3)
         load_wk(1, 1)
         for c in range(CHUNKS):
             load_res(c)
@@ -236,28 +250,35 @@ def tile_list_hwaytanhP_kernel(
             out=wv_codes[:].bitcast(U16).rearrange("p a (t m) -> p a t m", t=PACK),
             in_=wv_raw[:].bitcast(U16).rearrange("p a (m t) -> p a t m", t=PACK),
         )
-        gather(0, 0, 0, FIRST)
-        gather(0, 0, FIRST, J)
         nc.vector.tensor_copy(
             out=wv_scale[:].rearrange("p a (t m) -> p a t m", t=PACK),
             in_=wvs_raw[:].rearrange("p a (m t) -> p a t m", t=PACK),
         )
-        for i in range(1, PACK):
-            gather(0, i, 0, J)
-        first = [interleave("scalar", rows_of(0)[:, :, h * 512 : (h + 1) * 512], 512, "xb0", 2) for h in range(2)]
-        nc.vector.tensor_scalar(half_bias[:], bias[:], 0.5, None, ALU.mult)
+        gather(0, 0, 0, FIRST)
+        gather(0, 0, FIRST, J)
+        gather(0, 1, 0, J)
+        weave_pair("scalar", xb0, 0, 0, slice(0, J))
+        nc.scalar.mul(half_bias[:], bias[:], 0.5)
+        gather(0, 2, 0, J)
+        gather(0, 3, 0, J)
+        weave_pair("scalar", xb0, 0, 1, slice(0, J))
         gather(1, 0, 0, J)
-        quantize_xg(0, first[0], 0, 512)
         gather(1, 1, 0, J)
-        quantize_xg(0, first[1], 512, J)
+        xg_codes[0] = keep.tile([P, J], U32, name="xg_codes0", tag="x5", align_bytes=64)
+        quantize_xg(0, xb0, 0, J)
         deal_wk("scalar", 0, 0)
         deal_wk("scalar", 0, 1)
+        for c in range(CHUNKS):
+            weave_pair("scalar", xb1[c], 1, 0, cols_of(c))
         gather(1, 2, 0, J)
+        wk_codes[0] = keep.tile([P, N], U32, name="wk_codes0", tag="x0", align_bytes=64)
         quantize_wk(0)
 
         vb = {}
         kb = {}
-        xb = {}
+        tv = {}
+        diff = {}
+        y = {}
 
         def open_chunk(c):
             vb[c] = new_banks(c)
@@ -265,37 +286,15 @@ def tile_list_hwaytanhP_kernel(
             value_pass(vb[c], c, 0)
             key_pass(kb[c], c, 0)
 
-        def xg_chunk(engine, c):
-            xb[c] = interleave(engine, rows_of(1)[:, :, cols_of(c)], WIDTHS[c], "xb1", 4)
-
         def close_value(c):
-            quantize_xg(1, xb[c], STARTS[c], STARTS[c] + WIDTHS[c])
+            quantize_xg(1, xb1[c], STARTS[c], STARTS[c] + WIDTHS[c])
             value_pass(vb[c], c, 1)
-
-        def close_chunk(c):
-            close_value(c)
-            key_pass(kb[c], c, 1)
 
         def last_plane(c):
             gather(1, 3, STARTS[c], STARTS[c] + WIDTHS[c])
 
-        open_chunk(0)
-        open_chunk(1)
-        deal_wk("scalar", 1, 0)
-        last_plane(0)
-        last_plane(1)
-        xg_chunk("vector", 0)
-        xg_chunk("vector", 1)
-        close_value(0)
-        close_value(1)
-        deal_wk("vector", 1, 1)
-        last_plane(2)
-        quantize_wk(1)
-        key_pass(kb[0], 0, 1)
-        key_pass(kb[1], 1, 1)
-        gather(1, 3, STARTS[3], J)
-
-        tv = {}
+        def last_pair(c):
+            weave_pair("scalar", xb1[c], 1, 1, cols_of(c))
 
         def values(c):
             vb[c] = new_banks(c)
@@ -308,31 +307,50 @@ def tile_list_hwaytanhP_kernel(
             key_pass(kb[c], c, 0)
             key_pass(kb[c], c, 1)
 
-        xg_chunk("scalar", 2)
+        open_chunk(0)
+        open_chunk(1)
+        last_plane(0)
+        last_pair(0)
+        last_plane(1)
+        last_pair(1)
+        deal_wk("scalar", 1, 0)
+        last_plane(2)
+        gather(1, 3, STARTS[3], J)
+        close_value(0)
+        close_value(1)
+        deal_wk("vector", 1, 1)
         for c in range(2):
             tv[c] = value_tanh(vb[c], c)
-        diff = {0: difference(0, tv[0])}
+        quantize_wk(1)
+        key_pass(kb[0], 0, 1)
+        key_pass(kb[1], 1, 1)
+        last_pair(2)
+        diff[0] = difference(0, tv[0])
         values(2)
-        y = {}
+        last = CHUNKS - 1
+        th = {0: key_tanh(kb[0], 0)}
+        yb = {}
         for c in range(CHUNKS):
-            th = key_tanh(kb[c], c)
             if c + 3 < CHUNKS:
-                xg_chunk("scalar", c + 3)
+                last_pair(c + 3)
             if c + 2 < CHUNKS:
                 keys(c + 2)
-            if c + 1 < CHUNKS:
+            if c < last:
                 diff[c + 1] = difference(c + 1, tv[c + 1])
-            twice = gated(c, th, diff[c])
+                th[c + 1] = key_tanh(kb[c + 1], c + 1)
+            if c >= 2:
+                quantize_out(cols_of(c - 2), yb[c - 2])
+                store_codes(cols_of(c - 2))
+            twice = gated(c, th[c], diff[c])
             if c + 3 < CHUNKS:
                 values(c + 3)
+            if c >= 1:
+                yb[c - 1] = interleave("scalar", y[c - 1][:], WIDTHS[c - 1], "yb", 3)
             y[c] = finish(c, twice)
-        last = CHUNKS - 1
-        yb = {c: interleave("scalar", y[c][:], WIDTHS[c], "yb", 4) for c in range(last)}
-        for c in range(last - 1):
-            quantize_out(c, yb[c])
-        tail = interleave("vector", y[last][:], WIDTHS[last], "yb", 4)
-        quantize_out(last - 1, yb[last - 1])
-        quantize_out(last, tail)
+        quantize_out(cols_of(last - 1), yb[last - 1])
+        tail = interleave("vector", y[last][:], WIDTHS[last], "ye", 1)
+        quantize_out(cols_of(last), tail)
+        store_codes(slice(STARTS[last - 1], J))
 
         for q in range(4):
             eng = nc.sync if q % 2 == 0 else nc.scalar

@@ -102,8 +102,8 @@ def tile_list_hwaytanhP_kernel(
         def weave_pair(engine, dst, a, u, cols):
             copy_on(
                 engine,
-                dst[:].rearrange("p (c e i) -> p c i e", e=4, i=PACK)[:, :, 2 * u : 2 * u + 2, :],
-                rows_of(a)[:, 2 * u : 2 * u + 2, cols].rearrange("p i (c e) -> p c i e", e=4),
+                dst[:].rearrange("p (j i) -> p j i", i=PACK)[:, :, 2 * u : 2 * u + 2],
+                rows_of(a)[:, 2 * u : 2 * u + 2, cols].rearrange("p i j -> p j i"),
             )
 
         def quantize_xg(a, src, j0, j1):
@@ -223,13 +223,13 @@ def tile_list_hwaytanhP_kernel(
         nc.sync.dma_start(offsets[:], offs)
         nc.sync.dma_start(out=wv_raw[:].bitcast(I32), in_=wv_words.rearrange("a p b -> p a b").bitcast(I32))
         nc.sync.dma_start(out=weights[:, :FIRST], in_=wgt[:, :FIRST])
+        load_plane(0, 0)
+        nc.sync.dma_start(out=weights[:, FIRST:], in_=wgt[:, FIRST:])
         for q in range(4):
-            nc.sync.dma_start(
+            nc.scalar.dma_start(
                 out=wvs_raw[32 * q : 32 * q + 4, :, :].bitcast(I32),
                 in_=wv_scales[:, 4 * q : 4 * q + 4, :].rearrange("a r n -> r a n").bitcast(I32),
             )
-        load_plane(0, 0)
-        nc.sync.dma_start(out=weights[:, FIRST:], in_=wgt[:, FIRST:])
         nc.scalar.activation(out=warm[:, 4:5], in_=warm[:, 0:1], func=TANH)
         load_plane(0, 1)
         load_plane(0, 2)
@@ -250,12 +250,12 @@ def tile_list_hwaytanhP_kernel(
             out=wv_codes[:].bitcast(U16).rearrange("p a (t m) -> p a t m", t=PACK),
             in_=wv_raw[:].bitcast(U16).rearrange("p a (m t) -> p a t m", t=PACK),
         )
+        gather(0, 0, 0, FIRST)
+        gather(0, 0, FIRST, J)
         nc.vector.tensor_copy(
             out=wv_scale[:].rearrange("p a (t m) -> p a t m", t=PACK),
             in_=wvs_raw[:].rearrange("p a (m t) -> p a t m", t=PACK),
         )
-        gather(0, 0, 0, FIRST)
-        gather(0, 0, FIRST, J)
         gather(0, 1, 0, J)
         weave_pair("scalar", xb0, 0, 0, slice(0, J))
         nc.scalar.mul(half_bias[:], bias[:], 0.5)

@@ -166,14 +166,14 @@ def tile_list_hwaytanhP_kernel(
                 )
 
         def value_tanh(banks, c):
-            tv = work.tile([P, PACK * WIDTHS[c]], F32, name="tv", bufs=3)
+            tv = held("tv%d" % c, [P, PACK * WIDTHS[c]], F32)
             for u, bank in enumerate(banks):
                 nc.scalar.activation(out=tv[:, u * BANK : (u + 1) * BANK], in_=bank[:], func=TANH)
             return tv
 
         def key_tanh(banks, c):
             w = WIDTHS[c]
-            th = work.tile([P, PACK * w], F32, name="th", bufs=3)
+            th = held("th%d" % c, [P, PACK * w], F32)
             for t in range(PACK):
                 bank, lo, opens, closes = place(banks, c, t)
                 nc.scalar.activation(
@@ -189,7 +189,7 @@ def tile_list_hwaytanhP_kernel(
             return tile[:].rearrange("p t j -> p (t j)")
 
         def difference(c, tv):
-            diff = work.tile([P, PACK * WIDTHS[c]], F32, name="diff")
+            diff = work.tile([P, PACK * WIDTHS[c]], F32, name="diff", bufs=3)
             nc.vector.tensor_tensor(diff[:], tv[:], flat(carried[c]), ALU.subtract)
             return diff
 
@@ -199,7 +199,7 @@ def tile_list_hwaytanhP_kernel(
             return twice
 
         def finish(c, twice):
-            y = work.tile([P, PACK, WIDTHS[c]], F32, name="y", bufs=3)
+            y = held("y%d" % c, [P, PACK, WIDTHS[c]], F32)
             nc.vector.scalar_tensor_tensor(flat(y), twice[:], 0.5, flat(carried[c]), ALU.mult, ALU.add)
             rows = out_0.rearrange("(p t) j -> p t j", t=PACK)
             nc.sync.dma_start(out=rows[:, :, cols_of(c)], in_=y[:])
@@ -296,12 +296,6 @@ def tile_list_hwaytanhP_kernel(
         def last_pair(c):
             weave_pair("scalar", xb1[c], 1, 1, cols_of(c))
 
-        def values(c):
-            vb[c] = new_banks(c)
-            value_pass(vb[c], c, 0)
-            close_value(c)
-            tv[c] = value_tanh(vb[c], c)
-
         def keys(c):
             kb[c] = new_banks(c)
             key_pass(kb[c], c, 0)
@@ -324,29 +318,33 @@ def tile_list_hwaytanhP_kernel(
         quantize_wk(1)
         key_pass(kb[0], 0, 1)
         key_pass(kb[1], 1, 1)
-        last_pair(2)
         diff[0] = difference(0, tv[0])
-        values(2)
         last = CHUNKS - 1
-        th = {0: key_tanh(kb[0], 0)}
+        th = {}
+        for c in range(2, CHUNKS):
+            last_pair(c)
+            vb[c] = new_banks(c)
+            value_pass(vb[c], c, 0)
+            close_value(c)
+            if c == 2:
+                th[0] = key_tanh(kb[0], 0)
+            keys(c)
+            th[c - 1] = key_tanh(kb[c - 1], c - 1)
+            tv[c] = value_tanh(vb[c], c)
+        th[last] = key_tanh(kb[last], last)
+
         yb = {}
+        diff[1] = difference(1, tv[1])
         for c in range(CHUNKS):
-            if c + 3 < CHUNKS:
-                last_pair(c + 3)
-            if c + 2 < CHUNKS:
-                keys(c + 2)
-            if c < last:
+            twice = gated(c, th[c], diff[c])
+            if 1 <= c < last:
                 diff[c + 1] = difference(c + 1, tv[c + 1])
-                th[c + 1] = key_tanh(kb[c + 1], c + 1)
             if c >= 2:
                 quantize_out(cols_of(c - 2), yb[c - 2])
                 store_codes(cols_of(c - 2))
-            twice = gated(c, th[c], diff[c])
-            if c + 3 < CHUNKS:
-                values(c + 3)
-            if c >= 1:
-                yb[c - 1] = interleave("scalar", y[c - 1][:], WIDTHS[c - 1], "yb", 3)
             y[c] = finish(c, twice)
+            if c < last:
+                yb[c] = interleave("scalar", y[c][:], WIDTHS[c], "yb", 4)
         quantize_out(cols_of(last - 1), yb[last - 1])
         tail = interleave("vector", y[last][:], WIDTHS[last], "ye", 1)
         quantize_out(cols_of(last), tail)

@@ -20,11 +20,17 @@ P = 128
 PACK = 4
 K_PASS = P * PACK
 PASSES = K // K_PASS
+BANK = 512
+LIST = 16
+QUADRANTS = 4
+
 WIDTHS = [128, 256, 256, 256, 128]
 STARTS = [sum(WIDTHS[:c]) for c in range(len(WIDTHS))]
 CHUNKS = len(WIDTHS)
-BANK = 512
-LIST = 16
+LAST = CHUNKS - 1
+EARLY = 2
+FIRST_WEIGHTS = 256
+PLACE = [0, 1, 2, 3, 4, 5, 1, 2]
 
 
 def tile_list_hwaytanhP_kernel(
@@ -39,22 +45,21 @@ def tile_list_hwaytanhP_kernel(
         def held(name, shape, dtype):
             return keep.tile(shape, dtype, name=name, align_bytes=64)
 
+        def in_place_of(a, i, name, shape, dtype):
+            return keep.tile(shape, dtype, name=name, tag="place%d" % PLACE[PACK * a + i], align_bytes=64)
+
         offsets = held("offsets", [P, J // LIST], U16)
         wv_raw = held("wv_raw", [P, PASSES, 2 * N], U8)
         wvs_raw = held("wvs_raw", [P, PASSES, N], U8)
         wv_codes = held("wv_codes", [P, PASSES, 2 * N], U8)
-        wv_scale = held("wv_scale", [P, PASSES, N], U8)
         weights = held("weights", [P, J], F32)
         bias = held("bias", [P, PACK], F32)
         half_bias = held("half_bias", [P, PACK], F32)
-        planes = [
-            [keep.tile([P, T], F32, name="x", tag="x%d" % ((PACK * a + i) % 6), align_bytes=64) for i in range(PACK)]
-            for a in range(PASSES)
-        ]
+        planes = [[in_place_of(a, i, "plane", [P, T], F32) for i in range(PACK)] for a in range(PASSES)]
         picked = [held("picked%d" % a, [P, PACK * J], F32) for a in range(PASSES)]
         xg_codes = {1: held("xg_codes1", [P, J], U32)}
-        xb0 = held("xb0", [P, J * PACK], BF16)
-        xb1 = [held("xb1%d" % c, [P, WIDTHS[c] * PACK], BF16) for c in range(CHUNKS)]
+        woven_0 = held("woven_0", [P, J * PACK], BF16)
+        woven_1 = [held("woven_1%d" % c, [P, WIDTHS[c] * PACK], BF16) for c in range(CHUNKS)]
         xg_scale = [held("xg_scale%d" % a, [P, J], U8) for a in range(PASSES)]
         wk_raw = [[held("wk_raw%d%d" % (a, h), [P, PACK, N // 2], F32) for h in range(2)] for a in range(PASSES)]
         wk_bf = [held("wk_bf%d" % a, [P, PACK, P, PACK], BF16) for a in range(PASSES)]
@@ -63,7 +68,9 @@ def tile_list_hwaytanhP_kernel(
         carried = [held("carried%d" % c, [P, PACK, WIDTHS[c]], F32) for c in range(CHUNKS)]
         out_codes = held("out_codes", [P, J], U32)
         out_scale = held("out_scale", [P, J], U8)
-        warm = held("warm", [P, 8], F32)
+
+        def cols_of(c):
+            return slice(STARTS[c], STARTS[c] + WIDTHS[c])
 
         def load_plane(a, i):
             rows = xT[a * K_PASS : (a + 1) * K_PASS, :].rearrange("(p i) t -> p i t", i=PACK)
@@ -73,47 +80,32 @@ def tile_list_hwaytanhP_kernel(
             rows = wk[a * K_PASS : (a + 1) * K_PASS, :].rearrange("(p i) n -> p i n", i=PACK)
             nc.sync.dma_start(out=wk_raw[a][h][:], in_=rows[:, :, h * (N // 2) : (h + 1) * (N // 2)])
 
-        def rows_of(a):
-            return picked[a][:].rearrange("p (i j) -> p i j", i=PACK)
+        def load_res(c):
+            rows = res.rearrange("(p t) j -> p t j", t=PACK)
+            nc.sync.dma_start(out=carried[c][:], in_=rows[:, :, cols_of(c)])
 
-        def gather(a, i, j0, j1):
+        def gather(a, i, cols):
             nc.vector.tensor_tensor(
-                picked[a][:, i * J + j0 : i * J + j1],
-                planes[a][i][:].indirect(offsets[:, j0 // LIST : j1 // LIST]),
-                weights[:, j0:j1],
+                picked[a][:, i * J + cols.start : i * J + cols.stop],
+                planes[a][i][:].indirect(offsets[:, cols.start // LIST : cols.stop // LIST]),
+                weights[:, cols],
                 ALU.mult,
             )
 
-        def copy_on(engine, out, in_):
-            if engine == "vector":
-                nc.vector.tensor_copy(out=out, in_=in_)
-            else:
-                nc.scalar.copy(out=out, in_=in_)
-
-        def interleave(engine, src, width, tag, bufs):
-            dst = work.tile([P, width * PACK], BF16, name=tag, align_bytes=64, bufs=bufs)
-            copy_on(
-                engine,
-                dst[:].rearrange("p (c e i) -> p c i e", e=4, i=PACK),
-                src.rearrange("p i (c e) -> p c i e", e=4),
-            )
-            return dst
-
-        def weave_pair(engine, dst, a, u, cols):
-            copy_on(
-                engine,
-                dst[:].rearrange("p (j i) -> p j i", i=PACK)[:, :, 2 * u : 2 * u + 2],
-                rows_of(a)[:, 2 * u : 2 * u + 2, cols].rearrange("p i j -> p j i"),
+        def weave_pair(dst, a, u, cols):
+            rows = picked[a][:].rearrange("p (i j) -> p i j", i=PACK)
+            nc.scalar.copy(
+                out=dst[:].rearrange("p (j i) -> p j i", i=PACK)[:, :, 2 * u : 2 * u + 2],
+                in_=rows[:, 2 * u : 2 * u + 2, cols].rearrange("p i j -> p j i"),
             )
 
-        def quantize_xg(a, src, j0, j1):
-            nc.vector.quantize_mx(out=xg_codes[a][:, j0:j1].bitcast(FP8X4), scales=xg_scale[a][:, j0:j1], in_=src[:])
+        def quantize_xg(a, woven, cols):
+            nc.vector.quantize_mx(out=xg_codes[a][:, cols].bitcast(FP8X4), scales=xg_scale[a][:, cols], in_=woven[:])
 
-        def deal_wk(engine, a, h):
-            copy_on(
-                engine,
-                wk_bf[a][:, :, h * (P // 2) : (h + 1) * (P // 2), :].rearrange("p t m i -> p m i t"),
-                wk_raw[a][h][:].rearrange("p i (m t) -> p m i t", t=PACK),
+        def deal_wk(copy, a, h):
+            copy(
+                out=wk_bf[a][:, :, h * (P // 2) : (h + 1) * (P // 2), :].rearrange("p t m i -> p m i t"),
+                in_=wk_raw[a][h][:].rearrange("p i (m t) -> p m i t", t=PACK),
             )
 
         def quantize_wk(a):
@@ -123,12 +115,8 @@ def tile_list_hwaytanhP_kernel(
                 in_=wk_bf[a][:].rearrange("p t m i -> p (t m i)"),
             )
 
-        def cols_of(c):
-            return slice(STARTS[c], STARTS[c] + WIDTHS[c])
-
         def new_banks(c):
-            count = PACK * WIDTHS[c] // BANK
-            return [psum.tile([P, BANK], F32, name="bank") for u in range(count)]
+            return [psum.tile([P, BANK], F32, name="bank") for u in range(PACK * WIDTHS[c] // BANK)]
 
         def place(banks, c, t):
             per_bank = BANK // WIDTHS[c]
@@ -166,74 +154,76 @@ def tile_list_hwaytanhP_kernel(
                 )
 
         def value_tanh(banks, c):
-            tv = held("tv%d" % c, [P, PACK * WIDTHS[c]], F32)
+            result = held("tanh_ve%d" % c, [P, PACK * WIDTHS[c]], F32)
             for u, bank in enumerate(banks):
-                nc.scalar.activation(out=tv[:, u * BANK : (u + 1) * BANK], in_=bank[:], func=TANH)
-            return tv
+                nc.scalar.activation(out=result[:, u * BANK : (u + 1) * BANK], in_=bank[:], func=TANH)
+            return result
 
         def key_tanh(banks, c):
             w = WIDTHS[c]
-            th = held("th%d" % c, [P, PACK * w], F32)
+            result = held("tanh_ke%d" % c, [P, PACK * w], F32)
             for t in range(PACK):
                 bank, lo, opens, closes = place(banks, c, t)
                 nc.scalar.activation(
-                    out=th[:, t * w : (t + 1) * w],
+                    out=result[:, t * w : (t + 1) * w],
                     in_=bank[:, lo : lo + w],
                     func=TANH,
                     bias=half_bias[:, t : t + 1],
                     scale=0.5,
                 )
-            return th
+            return result
 
         def flat(tile):
             return tile[:].rearrange("p t j -> p (t j)")
 
-        def difference(c, tv):
-            diff = work.tile([P, PACK * WIDTHS[c]], F32, name="diff", bufs=3)
-            nc.vector.tensor_tensor(diff[:], tv[:], flat(carried[c]), ALU.subtract)
-            return diff
+        def difference(c):
+            result = work.tile([P, PACK * WIDTHS[c]], F32, name="diff", bufs=3)
+            nc.vector.tensor_tensor(result[:], tanh_ve[c][:], flat(carried[c]), ALU.subtract)
+            return result
 
-        def gated(c, th, diff):
-            twice = work.tile([P, PACK * WIDTHS[c]], F32, name="twice")
-            nc.vector.scalar_tensor_tensor(twice[:], th[:], 1.0, diff[:], ALU.add, ALU.mult)
-            return twice
+        def gated(c):
+            result = work.tile([P, PACK * WIDTHS[c]], F32, name="twice")
+            nc.vector.scalar_tensor_tensor(result[:], tanh_ke[c][:], 1.0, diff[c][:], ALU.add, ALU.mult)
+            return result
 
         def finish(c, twice):
-            y = held("y%d" % c, [P, PACK, WIDTHS[c]], F32)
-            nc.vector.scalar_tensor_tensor(flat(y), twice[:], 0.5, flat(carried[c]), ALU.mult, ALU.add)
+            result = held("y%d" % c, [P, PACK, WIDTHS[c]], F32)
+            nc.vector.scalar_tensor_tensor(flat(result), twice[:], 0.5, flat(carried[c]), ALU.mult, ALU.add)
             rows = out_0.rearrange("(p t) j -> p t j", t=PACK)
-            nc.sync.dma_start(out=rows[:, :, cols_of(c)], in_=y[:])
-            return y
+            nc.sync.dma_start(out=rows[:, :, cols_of(c)], in_=result[:])
+            return result
 
-        def quantize_out(cols, src):
-            nc.vector.quantize_mx(out=out_codes[:, cols].bitcast(FP8X4), scales=out_scale[:, cols], in_=src[:])
+        def weave_out(copy, c, y, name, bufs):
+            result = work.tile([P, WIDTHS[c] * PACK], BF16, name=name, align_bytes=64, bufs=bufs)
+            copy(
+                out=result[:].rearrange("p (c e t) -> p c t e", e=4, t=PACK),
+                in_=y[:].rearrange("p t (c e) -> p c t e", e=4),
+            )
+            return result
+
+        def quantize_out(c):
+            cols = cols_of(c)
+            nc.vector.quantize_mx(
+                out=out_codes[:, cols].bitcast(FP8X4), scales=out_scale[:, cols], in_=woven_out[c][:]
+            )
 
         def store_codes(cols):
             words = out_1[0].rearrange("p j t -> p (j t)").bitcast(I32)
             nc.sync.dma_start(out=words[:, cols], in_=out_codes[:, cols].bitcast(I32))
 
-        def load_res(c):
-            res_rows = res.rearrange("(p t) j -> p t j", t=PACK)
-            nc.sync.dma_start(out=carried[c][:], in_=res_rows[:, :, cols_of(c)])
-
-
-        FIRST = 256
         nc.vector.memset(wvs_raw[:].rearrange("p a n -> p (a n)").bitcast(I32), 0)
-        nc.vector.memset(warm[:], 0.0)
         nc.sync.dma_start(offsets[:], offs)
         nc.sync.dma_start(out=wv_raw[:].bitcast(I32), in_=wv_words.rearrange("a p b -> p a b").bitcast(I32))
-        nc.sync.dma_start(out=weights[:, :FIRST], in_=wgt[:, :FIRST])
+        nc.sync.dma_start(out=weights[:, :FIRST_WEIGHTS], in_=wgt[:, :FIRST_WEIGHTS])
         load_plane(0, 0)
-        nc.sync.dma_start(out=weights[:, FIRST:], in_=wgt[:, FIRST:])
-        for q in range(4):
+        nc.sync.dma_start(out=weights[:, FIRST_WEIGHTS:], in_=wgt[:, FIRST_WEIGHTS:])
+        for q in range(QUADRANTS):
             nc.scalar.dma_start(
                 out=wvs_raw[32 * q : 32 * q + 4, :, :].bitcast(I32),
                 in_=wv_scales[:, 4 * q : 4 * q + 4, :].rearrange("a r n -> r a n").bitcast(I32),
             )
-        nc.scalar.activation(out=warm[:, 4:5], in_=warm[:, 0:1], func=TANH)
-        load_plane(0, 1)
-        load_plane(0, 2)
-        load_plane(0, 3)
+        for i in range(1, PACK):
+            load_plane(0, i)
         nc.sync.dma_start(out=bias[:], in_=bg.rearrange("(p t) -> p t", t=PACK))
         load_plane(1, 0)
         load_plane(1, 1)
@@ -246,112 +236,97 @@ def tile_list_hwaytanhP_kernel(
         for c in range(CHUNKS):
             load_res(c)
 
+        whole = slice(0, J)
         nc.vector.tensor_copy(
             out=wv_codes[:].bitcast(U16).rearrange("p a (t m) -> p a t m", t=PACK),
             in_=wv_raw[:].bitcast(U16).rearrange("p a (m t) -> p a t m", t=PACK),
         )
-        gather(0, 0, 0, FIRST)
-        gather(0, 0, FIRST, J)
+        gather(0, 0, slice(0, FIRST_WEIGHTS))
+        gather(0, 0, slice(FIRST_WEIGHTS, J))
+        wv_scale = in_place_of(0, 0, "wv_scale", [P, PASSES, N], U8)
         nc.vector.tensor_copy(
             out=wv_scale[:].rearrange("p a (t m) -> p a t m", t=PACK),
             in_=wvs_raw[:].rearrange("p a (m t) -> p a t m", t=PACK),
         )
-        gather(0, 1, 0, J)
-        weave_pair("scalar", xb0, 0, 0, slice(0, J))
+        gather(0, 1, whole)
+        weave_pair(woven_0, 0, 0, whole)
         nc.scalar.mul(half_bias[:], bias[:], 0.5)
-        gather(0, 2, 0, J)
-        gather(0, 3, 0, J)
-        weave_pair("scalar", xb0, 0, 1, slice(0, J))
-        gather(1, 0, 0, J)
-        gather(1, 1, 0, J)
-        xg_codes[0] = keep.tile([P, J], U32, name="xg_codes0", tag="x5", align_bytes=64)
-        quantize_xg(0, xb0, 0, J)
-        deal_wk("scalar", 0, 0)
-        deal_wk("scalar", 0, 1)
+        gather(0, 2, whole)
+        gather(0, 3, whole)
+        weave_pair(woven_0, 0, 1, whole)
+        gather(1, 0, whole)
+        gather(1, 1, whole)
+        xg_codes[0] = in_place_of(1, 1, "xg_codes0", [P, J], U32)
+        quantize_xg(0, woven_0, whole)
+        deal_wk(nc.scalar.copy, 0, 0)
+        deal_wk(nc.scalar.copy, 0, 1)
         for c in range(CHUNKS):
-            weave_pair("scalar", xb1[c], 1, 0, cols_of(c))
-        gather(1, 2, 0, J)
-        wk_codes[0] = keep.tile([P, N], U32, name="wk_codes0", tag="x0", align_bytes=64)
+            weave_pair(woven_1[c], 1, 0, cols_of(c))
+        gather(1, 2, whole)
+        wk_codes[0] = in_place_of(1, 2, "wk_codes0", [P, N], U32)
         quantize_wk(0)
 
-        vb = {}
-        kb = {}
-        tv = {}
-        diff = {}
-        y = {}
-
-        def open_chunk(c):
-            vb[c] = new_banks(c)
-            kb[c] = new_banks(c)
-            value_pass(vb[c], c, 0)
-            key_pass(kb[c], c, 0)
+        value_banks = {}
+        key_banks = {}
+        for c in range(EARLY):
+            value_banks[c] = new_banks(c)
+            key_banks[c] = new_banks(c)
+            value_pass(value_banks[c], c, 0)
+            key_pass(key_banks[c], c, 0)
 
         def close_value(c):
-            quantize_xg(1, xb1[c], STARTS[c], STARTS[c] + WIDTHS[c])
-            value_pass(vb[c], c, 1)
+            quantize_xg(1, woven_1[c], cols_of(c))
+            value_pass(value_banks[c], c, 1)
 
-        def last_plane(c):
-            gather(1, 3, STARTS[c], STARTS[c] + WIDTHS[c])
-
-        def last_pair(c):
-            weave_pair("scalar", xb1[c], 1, 1, cols_of(c))
-
-        def keys(c):
-            kb[c] = new_banks(c)
-            key_pass(kb[c], c, 0)
-            key_pass(kb[c], c, 1)
-
-        open_chunk(0)
-        open_chunk(1)
-        last_plane(0)
-        last_pair(0)
-        last_plane(1)
-        last_pair(1)
-        deal_wk("scalar", 1, 0)
-        last_plane(2)
-        gather(1, 3, STARTS[3], J)
-        close_value(0)
-        close_value(1)
-        deal_wk("vector", 1, 1)
-        for c in range(2):
-            tv[c] = value_tanh(vb[c], c)
-        quantize_wk(1)
-        key_pass(kb[0], 0, 1)
-        key_pass(kb[1], 1, 1)
-        diff[0] = difference(0, tv[0])
-        last = CHUNKS - 1
-        th = {}
-        for c in range(2, CHUNKS):
-            last_pair(c)
-            vb[c] = new_banks(c)
-            value_pass(vb[c], c, 0)
+        for c in range(EARLY):
+            gather(1, 3, cols_of(c))
+            weave_pair(woven_1[c], 1, 1, cols_of(c))
+        deal_wk(nc.scalar.copy, 1, 0)
+        gather(1, 3, cols_of(EARLY))
+        gather(1, 3, slice(STARTS[EARLY + 1], J))
+        for c in range(EARLY):
             close_value(c)
-            if c == 2:
-                th[0] = key_tanh(kb[0], 0)
-            keys(c)
-            th[c - 1] = key_tanh(kb[c - 1], c - 1)
-            tv[c] = value_tanh(vb[c], c)
-        th[last] = key_tanh(kb[last], last)
+        deal_wk(nc.vector.tensor_copy, 1, 1)
+        tanh_ve = {c: value_tanh(value_banks[c], c) for c in range(EARLY)}
+        quantize_wk(1)
+        for c in range(EARLY):
+            key_pass(key_banks[c], c, 1)
+        diff = {0: difference(0)}
 
-        yb = {}
-        diff[1] = difference(1, tv[1])
+        tanh_ke = {}
+        for c in range(EARLY, CHUNKS):
+            weave_pair(woven_1[c], 1, 1, cols_of(c))
+            value_banks[c] = new_banks(c)
+            value_pass(value_banks[c], c, 0)
+            close_value(c)
+            if c == EARLY:
+                tanh_ke[0] = key_tanh(key_banks[0], 0)
+            key_banks[c] = new_banks(c)
+            key_pass(key_banks[c], c, 0)
+            key_pass(key_banks[c], c, 1)
+            tanh_ke[c - 1] = key_tanh(key_banks[c - 1], c - 1)
+            tanh_ve[c] = value_tanh(value_banks[c], c)
+        tanh_ke[LAST] = key_tanh(key_banks[LAST], LAST)
+
+        woven_out = {}
+        diff[1] = difference(1)
         for c in range(CHUNKS):
-            twice = gated(c, th[c], diff[c])
-            if 1 <= c < last:
-                diff[c + 1] = difference(c + 1, tv[c + 1])
+            twice = gated(c)
+            if 1 <= c < LAST:
+                diff[c + 1] = difference(c + 1)
             if c >= 2:
-                quantize_out(cols_of(c - 2), yb[c - 2])
+                quantize_out(c - 2)
                 store_codes(cols_of(c - 2))
-            y[c] = finish(c, twice)
-            if c < last:
-                yb[c] = interleave("scalar", y[c][:], WIDTHS[c], "yb", 4)
-        quantize_out(cols_of(last - 1), yb[last - 1])
-        tail = interleave("vector", y[last][:], WIDTHS[last], "ye", 1)
-        quantize_out(cols_of(last), tail)
-        store_codes(slice(STARTS[last - 1], J))
+            y = finish(c, twice)
+            if c < LAST:
+                woven_out[c] = weave_out(nc.scalar.copy, c, y, "woven_out", LAST)
+        quantize_out(LAST - 1)
+        woven_out[LAST] = weave_out(nc.vector.tensor_copy, LAST, y, "woven_last", 1)
+        quantize_out(LAST)
+        store_codes(slice(STARTS[LAST - 1], J))
 
-        for q in range(4):
-            eng = nc.sync if q % 2 == 0 else nc.scalar
-            eng.dma_start(
+        for q in range(QUADRANTS):
+            queue = nc.sync if q % 2 == 0 else nc.scalar
+            queue.dma_start(
                 out=out_2[0, 4 * q : 4 * q + 4, :].bitcast(I32), in_=out_scale[32 * q : 32 * q + 4, :].bitcast(I32)
             )

@@ -50,13 +50,14 @@ def tile_list_hwaytanhP_kernel(
 
         offsets = held("offsets", [P, J // LIST], U16)
         wv_raw = held("wv_raw", [P, PASSES, 2 * N], U8)
-        wvs_raw = held("wvs_raw", [P, PASSES, N], U8)
         wv_codes = held("wv_codes", [P, PASSES, 2 * N], U8)
         weights = held("weights", [P, J], F32)
         bias = held("bias", [P, PACK], F32)
         half_bias = held("half_bias", [P, PACK], F32)
         planes = [[in_place_of(a, i, "plane", [P, T], F32) for i in range(PACK)] for a in range(PASSES)]
+        wvs_raw = keep.tile([P, PASSES, N], U8, name="wvs_raw", tag="picked0", align_bytes=64)
         picked = [held("picked%d" % a, [P, PACK * J], F32) for a in range(PASSES)]
+        wv_scale = held("wv_scale", [P, PASSES, N], U8)
         xg_codes = {1: held("xg_codes1", [P, J], U32)}
         woven_0 = held("woven_0", [P, J * PACK], BF16)
         woven_1 = [held("woven_1%d" % c, [P, WIDTHS[c] * PACK], BF16) for c in range(CHUNKS)]
@@ -211,7 +212,7 @@ def tile_list_hwaytanhP_kernel(
             words = out_1[0].rearrange("p j t -> p (j t)").bitcast(I32)
             nc.sync.dma_start(out=words[:, cols], in_=out_codes[:, cols].bitcast(I32))
 
-        nc.vector.memset(wvs_raw[:].rearrange("p a n -> p (a n)").bitcast(I32), 0)
+        nc.gpsimd.memset(wvs_raw[:].rearrange("p a n -> p (a n)").bitcast(I32), 0)
         nc.sync.dma_start(offsets[:], offs)
         nc.sync.dma_start(out=wv_raw[:].bitcast(I32), in_=wv_words.rearrange("a p b -> p a b").bitcast(I32))
         nc.sync.dma_start(out=weights[:, :FIRST_WEIGHTS], in_=wgt[:, :FIRST_WEIGHTS])
@@ -241,13 +242,12 @@ def tile_list_hwaytanhP_kernel(
             out=wv_codes[:].bitcast(U16).rearrange("p a (t m) -> p a t m", t=PACK),
             in_=wv_raw[:].bitcast(U16).rearrange("p a (m t) -> p a t m", t=PACK),
         )
-        gather(0, 0, slice(0, FIRST_WEIGHTS))
-        gather(0, 0, slice(FIRST_WEIGHTS, J))
-        wv_scale = in_place_of(0, 0, "wv_scale", [P, PASSES, N], U8)
         nc.vector.tensor_copy(
             out=wv_scale[:].rearrange("p a (t m) -> p a t m", t=PACK),
             in_=wvs_raw[:].rearrange("p a (m t) -> p a t m", t=PACK),
         )
+        gather(0, 0, slice(0, FIRST_WEIGHTS))
+        gather(0, 0, slice(FIRST_WEIGHTS, J))
         gather(0, 1, whole)
         weave_pair(woven_0, 0, 0, whole)
         nc.scalar.mul(half_bias[:], bias[:], 0.5)

@@ -29,7 +29,6 @@ STARTS = [sum(WIDTHS[:c]) for c in range(len(WIDTHS))]
 CHUNKS = len(WIDTHS)
 LAST = CHUNKS - 1
 EARLY = 2
-FIRST_WEIGHTS = 256
 PLACE = [0, 1, 2, 3, 4, 5, 1, 2]
 
 
@@ -52,12 +51,14 @@ def tile_list_hwaytanhP_kernel(
         wv_raw = held("wv_raw", [P, PASSES, 2 * N], U8)
         wv_codes = held("wv_codes", [P, PASSES, 2 * N], U8)
         weights = held("weights", [P, J], F32)
+        compact = held("compact", [P, J // LIST], F32)
+        compact_turned = held("compact_turned", [P, J // LIST], F32)
+        repeated = keep.tile([P, J], F32, name="repeated", tag="picked1", align_bytes=64)
         bias = held("bias", [P, PACK], F32)
         half_bias = held("half_bias", [P, PACK], F32)
         planes = [[in_place_of(a, i, "plane", [P, T], F32) for i in range(PACK)] for a in range(PASSES)]
-        wvs_raw = keep.tile([P, PASSES, N], U8, name="wvs_raw", tag="picked0", align_bytes=64)
+        wvs_raw = held("wvs_raw", [P, PASSES, N], U8)
         picked = [held("picked%d" % a, [P, PACK * J], F32) for a in range(PASSES)]
-        wv_scale = held("wv_scale", [P, PASSES, N], U8)
         xg_codes = {1: held("xg_codes1", [P, J], U32)}
         woven_0 = held("woven_0", [P, J * PACK], BF16)
         woven_1 = [held("woven_1%d" % c, [P, WIDTHS[c] * PACK], BF16) for c in range(CHUNKS)]
@@ -214,21 +215,22 @@ def tile_list_hwaytanhP_kernel(
 
         nc.gpsimd.memset(wvs_raw[:].rearrange("p a n -> p (a n)").bitcast(I32), 0)
         nc.sync.dma_start(offsets[:], offs)
+        first_rows = wgt.rearrange("(g r) j -> g r j", r=LIST)[:, 0, :]
+        nc.sync.dma_start(out=compact[:], in_=first_rows.rearrange("g (c e) -> g c e", c=LIST))
         nc.sync.dma_start(out=wv_raw[:].bitcast(I32), in_=wv_words.rearrange("a p b -> p a b").bitcast(I32))
-        nc.sync.dma_start(out=weights[:, :FIRST_WEIGHTS], in_=wgt[:, :FIRST_WEIGHTS])
         load_plane(0, 0)
-        nc.sync.dma_start(out=weights[:, FIRST_WEIGHTS:], in_=wgt[:, FIRST_WEIGHTS:])
         for q in range(QUADRANTS):
-            nc.scalar.dma_start(
+            nc.sync.dma_start(
                 out=wvs_raw[32 * q : 32 * q + 4, :, :].bitcast(I32),
                 in_=wv_scales[:, 4 * q : 4 * q + 4, :].rearrange("a r n -> r a n").bitcast(I32),
             )
-        for i in range(1, PACK):
-            load_plane(0, i)
+        load_plane(0, 1)
+        load_plane(0, 2)
+        load_wk(0, 0)
+        load_plane(0, 3)
         nc.sync.dma_start(out=bias[:], in_=bg.rearrange("(p t) -> p t", t=PACK))
         load_plane(1, 0)
         load_plane(1, 1)
-        load_wk(0, 0)
         load_wk(0, 1)
         load_plane(1, 2)
         load_wk(1, 0)
@@ -238,19 +240,30 @@ def tile_list_hwaytanhP_kernel(
             load_res(c)
 
         whole = slice(0, J)
+        for b in range(2):
+            nc.vector.transpose(compact_turned[:, 32 * b : 32 * (b + 1)], compact[:, 32 * b : 32 * (b + 1)])
+        for h in range(2):
+            half = slice(h * J // 2, (h + 1) * J // 2)
+            source = compact_turned[:].rearrange("p (k c) -> p c k", c=LIST)[:, 8 * h : 8 * (h + 1), :]
+            nc.scalar.copy(
+                out=repeated[:, half].rearrange("p (c k r) -> p c k r", k=4, r=LIST),
+                in_=source.unsqueeze(3).to_broadcast([P, 8, 4, LIST]),
+            )
+            nc.vector.transpose(weights[:, half], repeated[:, half])
         nc.vector.tensor_copy(
             out=wv_codes[:].bitcast(U16).rearrange("p a (t m) -> p a t m", t=PACK),
             in_=wv_raw[:].bitcast(U16).rearrange("p a (m t) -> p a t m", t=PACK),
         )
+        gather(0, 0, whole)
+        wv_scale = in_place_of(0, 0, "wv_scale", [P, PASSES, N], U8)
         nc.vector.tensor_copy(
             out=wv_scale[:].rearrange("p a (t m) -> p a t m", t=PACK),
             in_=wvs_raw[:].rearrange("p a (m t) -> p a t m", t=PACK),
         )
-        gather(0, 0, slice(0, FIRST_WEIGHTS))
-        gather(0, 0, slice(FIRST_WEIGHTS, J))
         gather(0, 1, whole)
         weave_pair(woven_0, 0, 0, whole)
         nc.scalar.mul(half_bias[:], bias[:], 0.5)
+        deal_wk(nc.scalar.copy, 0, 0)
         gather(0, 2, whole)
         gather(0, 3, whole)
         weave_pair(woven_0, 0, 1, whole)
@@ -258,7 +271,6 @@ def tile_list_hwaytanhP_kernel(
         gather(1, 1, whole)
         xg_codes[0] = in_place_of(1, 1, "xg_codes0", [P, J], U32)
         quantize_xg(0, woven_0, whole)
-        deal_wk(nc.scalar.copy, 0, 0)
         deal_wk(nc.scalar.copy, 0, 1)
         for c in range(CHUNKS):
             weave_pair(woven_1[c], 1, 0, cols_of(c))

@@ -3,7 +3,9 @@ from contextlib import ExitStack
 import concourse.mybir as mybir
 
 K, N, T, J = 1024, 512, 2048, 1024
+HEADS = 8
 FLOPS = 2 * 2 * K * N * J
+BYTES = 4 * (K * T + HEADS * J + K * N + N + 2 * N * J) + K * N // 2 + K * N // 32 + N * J + N * J // 32 + 2 * HEADS * J
 
 F32 = mybir.dt.float32
 BF16 = mybir.dt.bfloat16
@@ -22,6 +24,8 @@ K_PASS = P * PACK
 PASSES = K // K_PASS
 BANK = 512
 LIST = 16
+GROUP = P // HEADS
+SQUARE = 32
 QUADRANTS = 4
 
 WIDTHS = [128, 256, 256, 256, 128]
@@ -51,13 +55,15 @@ def tile_list_hwaytanhP_kernel(
         wv_raw = held("wv_raw", [P, PASSES, 2 * N], U8)
         wv_codes = held("wv_codes", [P, PASSES, 2 * N], U8)
         weights = held("weights", [P, J], F32)
-        compact = held("compact", [P, J // LIST], F32)
-        compact_turned = held("compact_turned", [P, J // LIST], F32)
+        compact = held("compact", [P, J // GROUP], F32)
+        compact_turned = held("compact_turned", [P, J // GROUP], F32)
         repeated = keep.tile([P, J], F32, name="repeated", tag="picked1", align_bytes=64)
         bias = held("bias", [P, PACK], F32)
         half_bias = held("half_bias", [P, PACK], F32)
         planes = [[in_place_of(a, i, "plane", [P, T], F32) for i in range(PACK)] for a in range(PASSES)]
-        wvs_raw = held("wvs_raw", [P, PASSES, N], U8)
+        wvs_raw = held("wvs_raw", [P, N], U8)
+        wvs_dealt = held("wvs_dealt", [P, N], U8)
+        wv_scale = held("wv_scale", [P, PASSES, N], U8)
         picked = [held("picked%d" % a, [P, PACK * J], F32) for a in range(PASSES)]
         xg_codes = {1: held("xg_codes1", [P, J], U32)}
         woven_0 = held("woven_0", [P, J * PACK], BF16)
@@ -85,6 +91,22 @@ def tile_list_hwaytanhP_kernel(
         def load_res(c):
             rows = res.rearrange("(p t) j -> p t j", t=PACK)
             nc.sync.dma_start(out=carried[c][:], in_=rows[:, :, cols_of(c)])
+
+        def spread_weights():
+            squares = J // GROUP // SQUARE
+            for b in range(squares):
+                cols = slice(SQUARE * b, SQUARE * (b + 1))
+                nc.vector.transpose(compact_turned[:, cols], compact[:, cols])
+            runs = squares * SQUARE // GROUP
+            by_c = compact_turned[:].rearrange("p (k c) -> p c k", c=GROUP)
+            for h in range(2):
+                half = slice(h * J // 2, (h + 1) * J // 2)
+                source = by_c[:, h * GROUP // 2 : (h + 1) * GROUP // 2, :]
+                nc.scalar.copy(
+                    out=repeated[:, half].rearrange("p (c k r) -> p c k r", k=runs, r=GROUP),
+                    in_=source.unsqueeze(3).to_broadcast([P, GROUP // 2, runs, GROUP]),
+                )
+                nc.vector.transpose(weights[:, half], repeated[:, half])
 
         def gather(a, i, cols):
             nc.vector.tensor_tensor(
@@ -213,21 +235,18 @@ def tile_list_hwaytanhP_kernel(
             words = out_1[0].rearrange("p j t -> p (j t)").bitcast(I32)
             nc.sync.dma_start(out=words[:, cols], in_=out_codes[:, cols].bitcast(I32))
 
-        nc.gpsimd.memset(wvs_raw[:].rearrange("p a n -> p (a n)").bitcast(I32), 0)
+        nc.gpsimd.memset(wvs_raw[32:64, :].bitcast(I32), 0)
+        nc.gpsimd.memset(wvs_raw[64:, :].bitcast(I32), 0)
+        nc.gpsimd.memset(wv_scale[:].rearrange("p a n -> p (a n)").bitcast(I32), 0)
+
         nc.sync.dma_start(offsets[:], offs)
-        first_rows = wgt.rearrange("(g r) j -> g r j", r=LIST)[:, 0, :]
-        nc.sync.dma_start(out=compact[:], in_=first_rows.rearrange("g (c e) -> g c e", c=LIST))
+        first_rows = wgt.rearrange("(g r) j -> g r j", r=GROUP)[:, 0, :]
+        nc.sync.dma_start(out=compact[:], in_=first_rows.rearrange("g (c e) -> g c e", c=GROUP))
+        nc.sync.dma_start(out=wvs_raw[:32, :].bitcast(I32), in_=wv_scales.rearrange("a r n -> r a n").bitcast(I32))
         nc.sync.dma_start(out=wv_raw[:].bitcast(I32), in_=wv_words.rearrange("a p b -> p a b").bitcast(I32))
-        load_plane(0, 0)
-        for q in range(QUADRANTS):
-            nc.sync.dma_start(
-                out=wvs_raw[32 * q : 32 * q + 4, :, :].bitcast(I32),
-                in_=wv_scales[:, 4 * q : 4 * q + 4, :].rearrange("a r n -> r a n").bitcast(I32),
-            )
-        load_plane(0, 1)
-        load_plane(0, 2)
+        for i in range(PACK):
+            load_plane(0, i)
         load_wk(0, 0)
-        load_plane(0, 3)
         nc.sync.dma_start(out=bias[:], in_=bg.rearrange("(p t) -> p t", t=PACK))
         load_plane(1, 0)
         load_plane(1, 1)
@@ -239,27 +258,23 @@ def tile_list_hwaytanhP_kernel(
         for c in range(CHUNKS):
             load_res(c)
 
-        whole = slice(0, J)
-        for b in range(2):
-            nc.vector.transpose(compact_turned[:, 32 * b : 32 * (b + 1)], compact[:, 32 * b : 32 * (b + 1)])
-        for h in range(2):
-            half = slice(h * J // 2, (h + 1) * J // 2)
-            source = compact_turned[:].rearrange("p (k c) -> p c k", c=LIST)[:, 8 * h : 8 * (h + 1), :]
-            nc.scalar.copy(
-                out=repeated[:, half].rearrange("p (c k r) -> p c k r", k=4, r=LIST),
-                in_=source.unsqueeze(3).to_broadcast([P, 8, 4, LIST]),
-            )
-            nc.vector.transpose(weights[:, half], repeated[:, half])
+        spread_weights()
         nc.vector.tensor_copy(
             out=wv_codes[:].bitcast(U16).rearrange("p a (t m) -> p a t m", t=PACK),
             in_=wv_raw[:].bitcast(U16).rearrange("p a (m t) -> p a t m", t=PACK),
         )
-        gather(0, 0, whole)
-        wv_scale = in_place_of(0, 0, "wv_scale", [P, PASSES, N], U8)
         nc.vector.tensor_copy(
-            out=wv_scale[:].rearrange("p a (t m) -> p a t m", t=PACK),
-            in_=wvs_raw[:].rearrange("p a (m t) -> p a t m", t=PACK),
+            out=wvs_dealt[:].rearrange("p (t m) -> p t m", t=PACK),
+            in_=wvs_raw[:].rearrange("p (m t) -> p t m", t=PACK),
         )
+        for q in range(QUADRANTS):
+            nc.gpsimd.dma_start(
+                out=wv_scale[32 * q : 32 * q + 4, :, :].bitcast(I32),
+                in_=wvs_dealt[8 * q : 8 * q + 8, :].bitcast(I32),
+            )
+
+        whole = slice(0, J)
+        gather(0, 0, whole)
         gather(0, 1, whole)
         weave_pair(woven_0, 0, 0, whole)
         nc.scalar.mul(half_bias[:], bias[:], 0.5)
@@ -333,9 +348,10 @@ def tile_list_hwaytanhP_kernel(
             if c < LAST:
                 woven_out[c] = weave_out(nc.scalar.copy, c, y, "woven_out", LAST)
         quantize_out(LAST - 1)
+        store_codes(cols_of(LAST - 1))
         woven_out[LAST] = weave_out(nc.vector.tensor_copy, LAST, y, "woven_last", 1)
         quantize_out(LAST)
-        store_codes(slice(STARTS[LAST - 1], J))
+        store_codes(cols_of(LAST))
 
         for q in range(QUADRANTS):
             queue = nc.sync if q % 2 == 0 else nc.scalar

@@ -1,6 +1,7 @@
 from contextlib import ExitStack
 
 import concourse.mybir as mybir
+from concourse.masks import make_identity
 
 K, N, T, J = 1024, 512, 2048, 1024
 HEADS = 8
@@ -17,6 +18,7 @@ FP8X4 = mybir.dt.float8_e4m3fn_x4
 FP4X4 = mybir.dt.float4_e2m1fn_x4
 ALU = mybir.AluOpType
 TANH = mybir.ActivationFunctionType.Tanh
+COPY = mybir.ActivationFunctionType.Copy
 
 P = 128
 PACK = 4
@@ -34,6 +36,7 @@ CHUNKS = len(WIDTHS)
 LAST = CHUNKS - 1
 EARLY = 2
 PLACE = [0, 1, 2, 3, 4, 5, 1, 2]
+TURNED_PLACE = {3: 0, 4: 3}
 
 
 def tile_list_hwaytanhP_kernel(
@@ -116,9 +119,9 @@ def tile_list_hwaytanhP_kernel(
                 ALU.mult,
             )
 
-        def weave_pair(dst, a, u, cols):
+        def weave_pair(dst, a, u, cols, copy=nc.scalar.copy):
             rows = picked[a][:].rearrange("p (i j) -> p i j", i=PACK)
-            nc.scalar.copy(
+            copy(
                 out=dst[:].rearrange("p (j i) -> p j i", i=PACK)[:, :, 2 * u : 2 * u + 2],
                 in_=rows[:, 2 * u : 2 * u + 2, cols].rearrange("p i j -> p j i"),
             )
@@ -205,23 +208,75 @@ def tile_list_hwaytanhP_kernel(
             nc.vector.tensor_tensor(result[:], tanh_ve[c][:], flat(carried[c]), ALU.subtract)
             return result
 
+        def turn_res(c):
+            result = in_place_of(0, TURNED_PLACE[c], "res_turned", [P, PACK * WIDTHS[c]], F32)
+            for s in range(WIDTHS[c] // P):
+                bank = psum.tile([P, BANK], F32, name="bank")
+                for t in range(PACK):
+                    nc.tensor.transpose(
+                        bank[:, P * t : P * (t + 1)], carried[c][:, t, P * s : P * (s + 1)], identity[:]
+                    )
+                nc.scalar.activation(out=result[:, BANK * s : BANK * (s + 1)], in_=bank[:], func=COPY, scale=-1.0)
+            return result
+
+        def turned_value(c):
+            banks = new_banks(c)
+            for s, bank in enumerate(banks):
+                cols = slice(STARTS[c] + s * P, STARTS[c] + (s + 1) * P)
+                for a in range(PASSES):
+                    nc.tensor.matmul_mx(
+                        out=bank[:],
+                        lhsT=xg_codes[a][:, cols].bitcast(FP8X4),
+                        lhsT_scale=xg_scale[a][:, cols],
+                        rhs=wv_codes[:, a, :].bitcast(FP4X4),
+                        rhs_scale=wv_scale[:, a, :],
+                        start=(a == 0),
+                        stop=(a == PASSES - 1),
+                    )
+            return banks
+
+        def difference_in_psum(c):
+            banks = new_banks(c)
+            for t in range(PACK):
+                bank, lo, opens, closes = place(banks, c, t)
+                for s in range(WIDTHS[c] // P):
+                    cols = slice(BANK * s + P * t, BANK * s + P * (t + 1))
+                    for first, source in ((True, res_turned[c]), (False, tanh_ve[c])):
+                        nc.tensor.matmul(
+                            bank[:, lo + P * s : lo + P * (s + 1)],
+                            source[:, cols],
+                            identity[:],
+                            start=first,
+                            stop=not first,
+                            is_transpose=True,
+                        )
+            return banks
+
         def gated(c):
             result = work.tile([P, PACK * WIDTHS[c]], F32, name="twice")
-            nc.vector.scalar_tensor_tensor(result[:], tanh_ke[c][:], 1.0, diff[c][:], ALU.add, ALU.mult)
+            if c in TURNED_PLACE:
+                for u, bank in enumerate(diff[c]):
+                    cols = slice(u * BANK, (u + 1) * BANK)
+                    nc.vector.scalar_tensor_tensor(
+                        result[:, cols], tanh_ke[c][:, cols], 1.0, bank[:], ALU.add, ALU.mult
+                    )
+            else:
+                nc.vector.scalar_tensor_tensor(result[:], tanh_ke[c][:], 1.0, diff[c][:], ALU.add, ALU.mult)
             return result
 
         def finish(c, twice):
-            result = held("y%d" % c, [P, PACK, WIDTHS[c]], F32)
-            nc.vector.scalar_tensor_tensor(flat(result), twice[:], 0.5, flat(carried[c]), ALU.mult, ALU.add)
+            run = y_all[:, PACK * STARTS[c] : PACK * (STARTS[c] + WIDTHS[c])]
+            nc.vector.scalar_tensor_tensor(run, twice[:], 0.5, flat(carried[c]), ALU.mult, ALU.add)
+            result = run.rearrange("p (t j) -> p t j", t=PACK)
             rows = out_0.rearrange("(p t) j -> p t j", t=PACK)
-            nc.sync.dma_start(out=rows[:, :, cols_of(c)], in_=result[:])
+            nc.sync.dma_start(out=rows[:, :, cols_of(c)], in_=result)
             return result
 
         def weave_out(copy, c, y, name, bufs):
             result = work.tile([P, WIDTHS[c] * PACK], BF16, name=name, align_bytes=64, bufs=bufs)
             copy(
                 out=result[:].rearrange("p (c e t) -> p c t e", e=4, t=PACK),
-                in_=y[:].rearrange("p t (c e) -> p c t e", e=4),
+                in_=y.rearrange("p t (c e) -> p c t e", e=4),
             )
             return result
 
@@ -238,6 +293,8 @@ def tile_list_hwaytanhP_kernel(
         nc.gpsimd.memset(wvs_raw[32:64, :].bitcast(I32), 0)
         nc.gpsimd.memset(wvs_raw[64:, :].bitcast(I32), 0)
         nc.gpsimd.memset(wv_scale[:].rearrange("p a n -> p (a n)").bitcast(I32), 0)
+        identity = held("identity", [P, P], F32)
+        make_identity(nc, identity[:])
 
         nc.sync.dma_start(offsets[:], offs)
         first_rows = wgt.rearrange("(g r) j -> g r j", r=GROUP)[:, 0, :]
@@ -255,7 +312,7 @@ def tile_list_hwaytanhP_kernel(
         load_wk(1, 0)
         load_plane(1, 3)
         load_wk(1, 1)
-        for c in range(CHUNKS):
+        for c in (0, 1, 3, 4, 2):
             load_res(c)
 
         spread_weights()
@@ -311,6 +368,7 @@ def tile_list_hwaytanhP_kernel(
         deal_wk(nc.scalar.copy, 1, 0)
         gather(1, 3, cols_of(EARLY))
         gather(1, 3, slice(STARTS[EARLY + 1], J))
+        weave_pair(woven_1[EARLY], 1, 1, cols_of(EARLY))
         for c in range(EARLY):
             close_value(c)
         deal_wk(nc.vector.tensor_copy, 1, 1)
@@ -318,35 +376,50 @@ def tile_list_hwaytanhP_kernel(
         quantize_wk(1)
         for c in range(EARLY):
             key_pass(key_banks[c], c, 1)
+        quantize_xg(1, woven_1[EARLY], cols_of(EARLY))
+        for c in range(EARLY + 1, CHUNKS):
+            weave_pair(woven_1[c], 1, 1, cols_of(c), nc.vector.tensor_copy)
         diff = {0: difference(0)}
+        for c in range(EARLY + 1, CHUNKS):
+            quantize_xg(1, woven_1[c], cols_of(c))
 
         tanh_ke = {}
-        for c in range(EARLY, CHUNKS):
-            weave_pair(woven_1[c], 1, 1, cols_of(c))
-            value_banks[c] = new_banks(c)
-            value_pass(value_banks[c], c, 0)
-            close_value(c)
-            if c == EARLY:
-                tanh_ke[0] = key_tanh(key_banks[0], 0)
+        res_turned = {}
+
+        def key_products(c):
             key_banks[c] = new_banks(c)
             key_pass(key_banks[c], c, 0)
             key_pass(key_banks[c], c, 1)
+
+        value_banks[2] = new_banks(2)
+        value_pass(value_banks[2], 2, 0)
+        value_pass(value_banks[2], 2, 1)
+        tanh_ke[0] = key_tanh(key_banks[0], 0)
+        key_products(2)
+        tanh_ke[1] = key_tanh(key_banks[1], 1)
+        tanh_ve[2] = value_tanh(value_banks[2], 2)
+        for c in TURNED_PLACE:
+            value_banks[c] = turned_value(c)
             tanh_ke[c - 1] = key_tanh(key_banks[c - 1], c - 1)
+            res_turned[c] = turn_res(c)
+            key_products(c)
             tanh_ve[c] = value_tanh(value_banks[c], c)
+            diff[c] = difference_in_psum(c)
         tanh_ke[LAST] = key_tanh(key_banks[LAST], LAST)
 
         woven_out = {}
+        y_all = keep.tile([P, PACK * J], F32, name="y_all", tag="picked0", align_bytes=64)
         diff[1] = difference(1)
         for c in range(CHUNKS):
             twice = gated(c)
-            if 1 <= c < LAST:
+            if c == 1:
                 diff[c + 1] = difference(c + 1)
             if c >= 2:
                 quantize_out(c - 2)
                 store_codes(cols_of(c - 2))
             y = finish(c, twice)
             if c < LAST:
-                woven_out[c] = weave_out(nc.scalar.copy, c, y, "woven_out", LAST)
+                woven_out[c] = weave_out(nc.scalar.copy if c else nc.vector.tensor_copy, c, y, "woven_out", LAST)
         quantize_out(LAST - 1)
         store_codes(cols_of(LAST - 1))
         woven_out[LAST] = weave_out(nc.vector.tensor_copy, LAST, y, "woven_last", 1)

@@ -35,6 +35,9 @@ STARTS = [sum(WIDTHS[:c]) for c in range(len(WIDTHS))]
 CHUNKS = len(WIDTHS)
 LAST = CHUNKS - 1
 EARLY = 2
+PAIRED = 3
+FRONT = STARTS[PAIRED]
+REST = J - FRONT
 PLACE = [0, 1, 2, 3, 4, 5, 1, 2]
 TURNED_PLACE = {3: 0, 4: 3}
 
@@ -46,7 +49,7 @@ def tile_list_hwaytanhP_kernel(
     with ExitStack() as ctx:
         keep = ctx.enter_context(tc.tile_pool(name="keep", bufs=1))
         work = ctx.enter_context(tc.tile_pool(name="work", bufs=2))
-        psum = ctx.enter_context(tc.psum_pool(name="psum", bufs=8))
+        psum = ctx.enter_context(tc.psum_pool(name="psum", bufs=1))
 
         def held(name, shape, dtype):
             return keep.tile(shape, dtype, name=name, align_bytes=64)
@@ -67,14 +70,16 @@ def tile_list_hwaytanhP_kernel(
         wvs_raw = held("wvs_raw", [P, N], U8)
         wvs_dealt = held("wvs_dealt", [P, N], U8)
         wv_scale = held("wv_scale", [P, PASSES, N], U8)
-        picked = [held("picked%d" % a, [P, PACK * J], F32) for a in range(PASSES)]
+        picked = [held("picked0", [P, PACK * J], F32), held("picked1", [P, PACK * FRONT], F32)]
+        picked_rest = held("picked_rest", [P, 2 * REST + N * PACK // 2], F32)
         xg_codes = {1: held("xg_codes1", [P, J], U32)}
         woven_0 = held("woven_0", [P, J * PACK], BF16)
-        woven_1 = [held("woven_1%d" % c, [P, WIDTHS[c] * PACK], BF16) for c in range(CHUNKS)]
+        woven_1 = [held("woven_1%d" % c, [P, WIDTHS[c] * PACK], BF16) for c in range(PAIRED)]
+        woven_rest = held("woven_rest", [P, REST * PACK], BF16)
         xg_scale = [held("xg_scale%d" % a, [P, J], U8) for a in range(PASSES)]
         wk_raw = [[held("wk_raw%d%d" % (a, h), [P, PACK, N // 2], F32) for h in range(2)] for a in range(PASSES)]
-        wk_bf = [held("wk_bf%d" % a, [P, PACK, P, PACK], BF16) for a in range(PASSES)]
-        wk_codes = {1: held("wk_codes1", [P, N], U32)}
+        wk_bf = [held("wk_bf0", [P, N * PACK], BF16)[:], picked_rest[:, 2 * REST :].bitcast(BF16)]
+        wk_codes = [held("wk_codes%d" % a, [P, N], U32) for a in range(PASSES)]
         wk_scale = [held("wk_scale%d" % a, [P, N], U8) for a in range(PASSES)]
         carried = [held("carried%d" % c, [P, PACK, WIDTHS[c]], F32) for c in range(CHUNKS)]
         out_codes = held("out_codes", [P, J], U32)
@@ -111,27 +116,34 @@ def tile_list_hwaytanhP_kernel(
                 )
                 nc.vector.transpose(weights[:, half], repeated[:, half])
 
-        def gather(a, i, cols):
+        def gather(dst, a, i, cols):
             nc.vector.tensor_tensor(
-                picked[a][:, i * J + cols.start : i * J + cols.stop],
+                dst,
                 planes[a][i][:].indirect(offsets[:, cols.start // LIST : cols.stop // LIST]),
                 weights[:, cols],
                 ALU.mult,
             )
 
-        def weave_pair(dst, a, u, cols, copy=nc.scalar.copy):
+        def gather_front(a, i, cols):
+            width = (J, FRONT)[a]
+            gather(picked[a][:, i * width + cols.start : i * width + cols.stop], a, i, cols)
+
+        def gather_rest(i):
+            gather(picked_rest[:, i * REST : (i + 1) * REST], 1, i, slice(FRONT, J))
+
+        def weave_pair(dst, a, u, cols):
             rows = picked[a][:].rearrange("p (i j) -> p i j", i=PACK)
-            copy(
+            nc.scalar.copy(
                 out=dst[:].rearrange("p (j i) -> p j i", i=PACK)[:, :, 2 * u : 2 * u + 2],
                 in_=rows[:, 2 * u : 2 * u + 2, cols].rearrange("p i j -> p j i"),
             )
 
         def quantize_xg(a, woven, cols):
-            nc.vector.quantize_mx(out=xg_codes[a][:, cols].bitcast(FP8X4), scales=xg_scale[a][:, cols], in_=woven[:])
+            nc.vector.quantize_mx(out=xg_codes[a][:, cols].bitcast(FP8X4), scales=xg_scale[a][:, cols], in_=woven)
 
         def deal_wk(copy, a, h):
             copy(
-                out=wk_bf[a][:, :, h * (P // 2) : (h + 1) * (P // 2), :].rearrange("p t m i -> p m i t"),
+                out=wk_bf[a].rearrange("p (t m i) -> p m i t", t=PACK, i=PACK)[:, h * (P // 2) : (h + 1) * (P // 2)],
                 in_=wk_raw[a][h][:].rearrange("p i (m t) -> p m i t", t=PACK),
             )
 
@@ -139,11 +151,11 @@ def tile_list_hwaytanhP_kernel(
             nc.vector.quantize_mx(
                 out=wk_codes[a][:].bitcast(FP8X4),
                 scales=wk_scale[a][:],
-                in_=wk_bf[a][:].rearrange("p t m i -> p (t m i)"),
+                in_=wk_bf[a],
             )
 
-        def new_banks(c):
-            return [psum.tile([P, BANK], F32, name="bank") for u in range(PACK * WIDTHS[c] // BANK)]
+        def take(*numbers):
+            return [psum.tile([P, BANK], F32, name="bank%d" % u) for u in numbers]
 
         def place(banks, c, t):
             per_bank = BANK // WIDTHS[c]
@@ -208,19 +220,21 @@ def tile_list_hwaytanhP_kernel(
             nc.vector.tensor_tensor(result[:], tanh_ve[c][:], flat(carried[c]), ALU.subtract)
             return result
 
-        def turn_res(c):
-            result = in_place_of(0, TURNED_PLACE[c], "res_turned", [P, PACK * WIDTHS[c]], F32)
-            for s in range(WIDTHS[c] // P):
-                bank = psum.tile([P, BANK], F32, name="bank")
+        def turn_res(banks, c):
+            for s, bank in enumerate(banks):
                 for t in range(PACK):
                     nc.tensor.transpose(
                         bank[:, P * t : P * (t + 1)], carried[c][:, t, P * s : P * (s + 1)], identity[:]
                     )
+            return banks
+
+        def negate(banks, c):
+            result = in_place_of(0, TURNED_PLACE[c], "res_turned", [P, PACK * WIDTHS[c]], F32)
+            for s, bank in enumerate(banks):
                 nc.scalar.activation(out=result[:, BANK * s : BANK * (s + 1)], in_=bank[:], func=COPY, scale=-1.0)
             return result
 
-        def turned_value(c):
-            banks = new_banks(c)
+        def turned_value(banks, c):
             for s, bank in enumerate(banks):
                 cols = slice(STARTS[c] + s * P, STARTS[c] + (s + 1) * P)
                 for a in range(PASSES):
@@ -235,30 +249,30 @@ def tile_list_hwaytanhP_kernel(
                     )
             return banks
 
-        def difference_in_psum(c):
-            banks = new_banks(c)
-            for t in range(PACK):
-                bank, lo, opens, closes = place(banks, c, t)
-                for s in range(WIDTHS[c] // P):
-                    cols = slice(BANK * s + P * t, BANK * s + P * (t + 1))
-                    for first, source in ((True, res_turned[c]), (False, tanh_ve[c])):
-                        nc.tensor.matmul(
-                            bank[:, lo + P * s : lo + P * (s + 1)],
-                            source[:, cols],
-                            identity[:],
-                            start=first,
-                            stop=not first,
-                            is_transpose=True,
-                        )
-            return banks
+        def add_turned(banks, source, first):
+            for s, bank in enumerate(banks):
+                for t in range(PACK):
+                    nc.tensor.matmul(
+                        bank[:, P * t : P * (t + 1)],
+                        source[:, BANK * s + P * t : BANK * s + P * (t + 1)],
+                        identity[:],
+                        start=(first and t == 0),
+                        stop=(not first and t == PACK - 1),
+                        is_transpose=True,
+                    )
 
         def gated(c):
             result = work.tile([P, PACK * WIDTHS[c]], F32, name="twice")
             if c in TURNED_PLACE:
-                for u, bank in enumerate(diff[c]):
-                    cols = slice(u * BANK, (u + 1) * BANK)
+                for s, bank in enumerate(diff[c]):
+                    cols = slice(s * P, (s + 1) * P)
                     nc.vector.scalar_tensor_tensor(
-                        result[:, cols], tanh_ke[c][:, cols], 1.0, bank[:], ALU.add, ALU.mult
+                        result[:].rearrange("p (t j) -> p t j", t=PACK)[:, :, cols],
+                        tanh_ke[c][:].rearrange("p (t j) -> p t j", t=PACK)[:, :, cols],
+                        1.0,
+                        bank[:].rearrange("p (t j) -> p t j", t=PACK),
+                        ALU.add,
+                        ALU.mult,
                     )
             else:
                 nc.vector.scalar_tensor_tensor(result[:], tanh_ke[c][:], 1.0, diff[c][:], ALU.add, ALU.mult)
@@ -331,44 +345,41 @@ def tile_list_hwaytanhP_kernel(
             )
 
         whole = slice(0, J)
-        gather(0, 0, whole)
-        gather(0, 1, whole)
+        front = slice(0, FRONT)
+        gather_front(0, 0, whole)
+        gather_front(0, 1, whole)
         weave_pair(woven_0, 0, 0, whole)
         nc.scalar.mul(half_bias[:], bias[:], 0.5)
         deal_wk(nc.scalar.copy, 0, 0)
-        gather(0, 2, whole)
-        gather(0, 3, whole)
+        gather_front(0, 2, whole)
+        gather_front(0, 3, whole)
         weave_pair(woven_0, 0, 1, whole)
-        gather(1, 0, whole)
-        gather(1, 1, whole)
+        for i in range(2):
+            gather_front(1, i, front)
+            gather_rest(i)
         xg_codes[0] = in_place_of(1, 1, "xg_codes0", [P, J], U32)
-        quantize_xg(0, woven_0, whole)
+        quantize_xg(0, woven_0[:], whole)
         deal_wk(nc.scalar.copy, 0, 1)
-        for c in range(CHUNKS):
+        for c in range(PAIRED):
             weave_pair(woven_1[c], 1, 0, cols_of(c))
-        gather(1, 2, whole)
-        wk_codes[0] = in_place_of(1, 2, "wk_codes0", [P, N], U32)
         quantize_wk(0)
+        gather_front(1, 2, front)
+        deal_wk(nc.scalar.copy, 1, 0)
 
-        value_banks = {}
-        key_banks = {}
+        value_banks = {0: take(0), 1: take(2, 3), 2: take(6, 7)}
+        key_banks = {0: take(1), 1: take(4, 5)}
         for c in range(EARLY):
-            value_banks[c] = new_banks(c)
-            key_banks[c] = new_banks(c)
             value_pass(value_banks[c], c, 0)
             key_pass(key_banks[c], c, 0)
+        value_pass(value_banks[2], 2, 0)
 
         def close_value(c):
-            quantize_xg(1, woven_1[c], cols_of(c))
+            quantize_xg(1, woven_1[c][:], cols_of(c))
             value_pass(value_banks[c], c, 1)
 
-        for c in range(EARLY):
-            gather(1, 3, cols_of(c))
+        for c in range(PAIRED):
+            gather_front(1, 3, cols_of(c))
             weave_pair(woven_1[c], 1, 1, cols_of(c))
-        deal_wk(nc.scalar.copy, 1, 0)
-        gather(1, 3, cols_of(EARLY))
-        gather(1, 3, slice(STARTS[EARLY + 1], J))
-        weave_pair(woven_1[EARLY], 1, 1, cols_of(EARLY))
         for c in range(EARLY):
             close_value(c)
         deal_wk(nc.vector.tensor_copy, 1, 1)
@@ -376,40 +387,53 @@ def tile_list_hwaytanhP_kernel(
         quantize_wk(1)
         for c in range(EARLY):
             key_pass(key_banks[c], c, 1)
-        quantize_xg(1, woven_1[EARLY], cols_of(EARLY))
-        for c in range(EARLY + 1, CHUNKS):
-            weave_pair(woven_1[c], 1, 1, cols_of(c), nc.vector.tensor_copy)
+        close_value(2)
+        gather_rest(2)
+        gather_rest(3)
         diff = {0: difference(0)}
-        for c in range(EARLY + 1, CHUNKS):
-            quantize_xg(1, woven_1[c], cols_of(c))
+        nc.vector.tensor_copy(
+            out=woven_rest[:].rearrange("p (c e i) -> p c i e", e=4, i=PACK),
+            in_=picked_rest[:, : PACK * REST].rearrange("p (i c e) -> p c i e", e=4, i=PACK),
+        )
+        diff[1] = difference(1)
+        for c in range(PAIRED, CHUNKS):
+            lo = PACK * (STARTS[c] - FRONT)
+            quantize_xg(1, woven_rest[:, lo : lo + PACK * WIDTHS[c]], cols_of(c))
 
         tanh_ke = {}
         res_turned = {}
 
-        def key_products(c):
-            key_banks[c] = new_banks(c)
-            key_pass(key_banks[c], c, 0)
-            key_pass(key_banks[c], c, 1)
+        def key_products(banks, c):
+            key_banks[c] = banks
+            key_pass(banks, c, 0)
+            key_pass(banks, c, 1)
 
-        value_banks[2] = new_banks(2)
-        value_pass(value_banks[2], 2, 0)
-        value_pass(value_banks[2], 2, 1)
         tanh_ke[0] = key_tanh(key_banks[0], 0)
-        key_products(2)
+        key_products(take(0, 2), 2)
         tanh_ke[1] = key_tanh(key_banks[1], 1)
         tanh_ve[2] = value_tanh(value_banks[2], 2)
-        for c in TURNED_PLACE:
-            value_banks[c] = turned_value(c)
-            tanh_ke[c - 1] = key_tanh(key_banks[c - 1], c - 1)
-            res_turned[c] = turn_res(c)
-            key_products(c)
-            tanh_ve[c] = value_tanh(value_banks[c], c)
-            diff[c] = difference_in_psum(c)
-        tanh_ke[LAST] = key_tanh(key_banks[LAST], LAST)
+        res_banks = turn_res(take(4, 5), 3)
+        value_banks[3] = turned_value(take(3, 1), 3)
+        res_turned[3] = negate(res_banks, 3)
+        key_products(take(6, 7), 3)
+        tanh_ke[2] = key_tanh(key_banks[2], 2)
+        value_banks[4] = turned_value(take(4), 4)
+        res_banks = turn_res(take(5), 4)
+        diff[3] = take(0, 2)
+        add_turned(diff[3], res_turned[3], True)
+        tanh_ve[3] = value_tanh(value_banks[3], 3)
+        key_products(take(3), 4)
+        add_turned(diff[3], tanh_ve[3], False)
+        tanh_ke[3] = key_tanh(key_banks[3], 3)
+        res_turned[4] = negate(res_banks, 4)
+        diff[4] = take(1)
+        add_turned(diff[4], res_turned[4], True)
+        tanh_ve[4] = value_tanh(value_banks[4], 4)
+        add_turned(diff[4], tanh_ve[4], False)
+        tanh_ke[4] = key_tanh(key_banks[4], 4)
 
         woven_out = {}
         y_all = keep.tile([P, PACK * J], F32, name="y_all", tag="picked0", align_bytes=64)
-        diff[1] = difference(1)
         for c in range(CHUNKS):
             twice = gated(c)
             if c == 1:
@@ -419,7 +443,7 @@ def tile_list_hwaytanhP_kernel(
                 store_codes(cols_of(c - 2))
             y = finish(c, twice)
             if c < LAST:
-                woven_out[c] = weave_out(nc.scalar.copy if c else nc.vector.tensor_copy, c, y, "woven_out", LAST)
+                woven_out[c] = weave_out(nc.scalar.copy, c, y, "woven_out", LAST)
         quantize_out(LAST - 1)
         store_codes(cols_of(LAST - 1))
         woven_out[LAST] = weave_out(nc.vector.tensor_copy, LAST, y, "woven_last", 1)

@@ -107,14 +107,14 @@ def tile_list_hwaytanhP_kernel(
                 nc.vector.transpose(compact_turned[:, cols], compact[:, cols])
             runs = squares * SQUARE // GROUP
             by_c = compact_turned[:].rearrange("p (k c) -> p c k", c=GROUP)
-            for h in range(2):
-                half = slice(h * J // 2, (h + 1) * J // 2)
-                source = by_c[:, h * GROUP // 2 : (h + 1) * GROUP // 2, :]
+            for h in range(4):
+                part = slice(h * J // 4, (h + 1) * J // 4)
+                source = by_c[:, h * GROUP // 4 : (h + 1) * GROUP // 4, :]
                 nc.scalar.copy(
-                    out=repeated[:, half].rearrange("p (c k r) -> p c k r", k=runs, r=GROUP),
-                    in_=source.unsqueeze(3).to_broadcast([P, GROUP // 2, runs, GROUP]),
+                    out=repeated[:, part].rearrange("p (c k r) -> p c k r", k=runs, r=GROUP),
+                    in_=source.unsqueeze(3).to_broadcast([P, GROUP // 4, runs, GROUP]),
                 )
-                nc.vector.transpose(weights[:, half], repeated[:, half])
+                nc.vector.transpose(weights[:, part], repeated[:, part])
 
         def gather(dst, a, i, cols):
             nc.vector.tensor_tensor(
@@ -312,14 +312,14 @@ def tile_list_hwaytanhP_kernel(
 
         nc.sync.dma_start(offsets[:], offs)
         first_rows = wgt.rearrange("(g r) j -> g r j", r=GROUP)[:, 0, :]
-        nc.sync.dma_start(out=compact[:], in_=first_rows.rearrange("g (c e) -> g c e", c=GROUP))
+        nc.scalar.dma_start(out=compact[:], in_=first_rows.rearrange("g (c e) -> g c e", c=GROUP))
         nc.sync.dma_start(out=wvs_raw[:32, :].bitcast(I32), in_=wv_scales.rearrange("a r n -> r a n").bitcast(I32))
-        nc.sync.dma_start(out=wv_raw[:].bitcast(I32), in_=wv_words.rearrange("a p b -> p a b").bitcast(I32))
         for i in range(PACK):
             load_plane(0, i)
         load_wk(0, 0)
         nc.sync.dma_start(out=bias[:], in_=bg.rearrange("(p t) -> p t", t=PACK))
         load_plane(1, 0)
+        nc.sync.dma_start(out=wv_raw[:].bitcast(I32), in_=wv_words.rearrange("a p b -> p a b").bitcast(I32))
         load_plane(1, 1)
         load_wk(0, 1)
         load_plane(1, 2)
@@ -330,10 +330,6 @@ def tile_list_hwaytanhP_kernel(
             load_res(c)
 
         spread_weights()
-        nc.vector.tensor_copy(
-            out=wv_codes[:].bitcast(U16).rearrange("p a (t m) -> p a t m", t=PACK),
-            in_=wv_raw[:].bitcast(U16).rearrange("p a (m t) -> p a t m", t=PACK),
-        )
         nc.vector.tensor_copy(
             out=wvs_dealt[:].rearrange("p (t m) -> p t m", t=PACK),
             in_=wvs_raw[:].rearrange("p (m t) -> p t m", t=PACK),
@@ -354,6 +350,10 @@ def tile_list_hwaytanhP_kernel(
         gather_front(0, 2, whole)
         gather_front(0, 3, whole)
         weave_pair(woven_0, 0, 1, whole)
+        nc.scalar.copy(
+            out=wv_codes[:].bitcast(U16).rearrange("p a (t m) -> p a t m", t=PACK),
+            in_=wv_raw[:].bitcast(U16).rearrange("p a (m t) -> p a t m", t=PACK),
+        )
         for i in range(2):
             gather_front(1, i, front)
             gather_rest(i)

@@ -314,12 +314,13 @@ def tile_list_hwaytanhP_kernel(
         first_rows = wgt.rearrange("(g r) j -> g r j", r=GROUP)[:, 0, :]
         nc.scalar.dma_start(out=compact[:], in_=first_rows.rearrange("g (c e) -> g c e", c=GROUP))
         nc.sync.dma_start(out=wvs_raw[:32, :].bitcast(I32), in_=wv_scales.rearrange("a r n -> r a n").bitcast(I32))
-        for i in range(PACK):
+        load_plane(0, 0)
+        nc.sync.dma_start(out=wv_raw[:].bitcast(I32), in_=wv_words.rearrange("a p b -> p a b").bitcast(I32))
+        for i in range(1, PACK):
             load_plane(0, i)
         load_wk(0, 0)
         nc.sync.dma_start(out=bias[:], in_=bg.rearrange("(p t) -> p t", t=PACK))
         load_plane(1, 0)
-        nc.sync.dma_start(out=wv_raw[:].bitcast(I32), in_=wv_words.rearrange("a p b -> p a b").bitcast(I32))
         load_plane(1, 1)
         load_wk(0, 1)
         load_plane(1, 2)
@@ -330,6 +331,10 @@ def tile_list_hwaytanhP_kernel(
             load_res(c)
 
         spread_weights()
+        nc.scalar.copy(
+            out=wv_codes[:].bitcast(U16).rearrange("p a (t m) -> p a t m", t=PACK),
+            in_=wv_raw[:].bitcast(U16).rearrange("p a (m t) -> p a t m", t=PACK),
+        )
         nc.vector.tensor_copy(
             out=wvs_dealt[:].rearrange("p (t m) -> p t m", t=PACK),
             in_=wvs_raw[:].rearrange("p (m t) -> p t m", t=PACK),
@@ -350,10 +355,6 @@ def tile_list_hwaytanhP_kernel(
         gather_front(0, 2, whole)
         gather_front(0, 3, whole)
         weave_pair(woven_0, 0, 1, whole)
-        nc.scalar.copy(
-            out=wv_codes[:].bitcast(U16).rearrange("p a (t m) -> p a t m", t=PACK),
-            in_=wv_raw[:].bitcast(U16).rearrange("p a (m t) -> p a t m", t=PACK),
-        )
         for i in range(2):
             gather_front(1, i, front)
             gather_rest(i)

@@ -71,14 +71,13 @@ def tile_list_hwaytanhP_kernel(
         wvs_dealt = held("wvs_dealt", [P, N], U8)
         wv_scale = held("wv_scale", [P, PASSES, N], U8)
         picked = [held("picked0", [P, PACK * J], F32), held("picked1", [P, PACK * FRONT], F32)]
-        picked_rest = held("picked_rest", [P, 2 * REST + N * PACK // 2], F32)
+        picked_rest = held("picked_rest", [P, 3 * REST + N * PACK // 2], F32)
         xg_codes = {1: held("xg_codes1", [P, J], U32)}
         woven_0 = held("woven_0", [P, J * PACK], BF16)
-        woven_1 = [held("woven_1%d" % c, [P, WIDTHS[c] * PACK], BF16) for c in range(PAIRED)]
         woven_rest = held("woven_rest", [P, REST * PACK], BF16)
         xg_scale = [held("xg_scale%d" % a, [P, J], U8) for a in range(PASSES)]
         wk_raw = [[held("wk_raw%d%d" % (a, h), [P, PACK, N // 2], F32) for h in range(2)] for a in range(PASSES)]
-        wk_bf = [held("wk_bf0", [P, N * PACK], BF16)[:], picked_rest[:, 2 * REST :].bitcast(BF16)]
+        wk_bf = [held("wk_bf0", [P, N * PACK], BF16)[:], picked_rest[:, 3 * REST :].bitcast(BF16)]
         wk_codes = [held("wk_codes%d" % a, [P, N], U32) for a in range(PASSES)]
         wk_scale = [held("wk_scale%d" % a, [P, N], U8) for a in range(PASSES)]
         carried = [held("carried%d" % c, [P, PACK, WIDTHS[c]], F32) for c in range(CHUNKS)]
@@ -318,12 +317,12 @@ def tile_list_hwaytanhP_kernel(
         nc.sync.dma_start(out=wv_raw[:].bitcast(I32), in_=wv_words.rearrange("a p b -> p a b").bitcast(I32))
         for i in range(1, PACK):
             load_plane(0, i)
-        load_wk(0, 0)
-        nc.sync.dma_start(out=bias[:], in_=bg.rearrange("(p t) -> p t", t=PACK))
         load_plane(1, 0)
         load_plane(1, 1)
-        load_wk(0, 1)
+        nc.sync.dma_start(out=bias[:], in_=bg.rearrange("(p t) -> p t", t=PACK))
+        load_wk(0, 0)
         load_plane(1, 2)
+        load_wk(0, 1)
         load_wk(1, 0)
         load_plane(1, 3)
         load_wk(1, 1)
@@ -331,10 +330,6 @@ def tile_list_hwaytanhP_kernel(
             load_res(c)
 
         spread_weights()
-        nc.scalar.copy(
-            out=wv_codes[:].bitcast(U16).rearrange("p a (t m) -> p a t m", t=PACK),
-            in_=wv_raw[:].bitcast(U16).rearrange("p a (m t) -> p a t m", t=PACK),
-        )
         nc.vector.tensor_copy(
             out=wvs_dealt[:].rearrange("p (t m) -> p t m", t=PACK),
             in_=wvs_raw[:].rearrange("p (m t) -> p t m", t=PACK),
@@ -348,31 +343,37 @@ def tile_list_hwaytanhP_kernel(
         whole = slice(0, J)
         front = slice(0, FRONT)
         gather_front(0, 0, whole)
+        nc.vector.tensor_copy(
+            out=wv_codes[:].bitcast(U16).rearrange("p a (t m) -> p a t m", t=PACK),
+            in_=wv_raw[:].bitcast(U16).rearrange("p a (m t) -> p a t m", t=PACK),
+        )
         gather_front(0, 1, whole)
         weave_pair(woven_0, 0, 0, whole)
-        nc.scalar.mul(half_bias[:], bias[:], 0.5)
-        deal_wk(nc.scalar.copy, 0, 0)
         gather_front(0, 2, whole)
         gather_front(0, 3, whole)
         weave_pair(woven_0, 0, 1, whole)
+        nc.scalar.mul(half_bias[:], bias[:], 0.5)
+        deal_wk(nc.scalar.copy, 0, 0)
         for i in range(2):
             gather_front(1, i, front)
             gather_rest(i)
         xg_codes[0] = in_place_of(1, 1, "xg_codes0", [P, J], U32)
         quantize_xg(0, woven_0[:], whole)
+        woven_front = keep.tile([P, FRONT * PACK], BF16, name="woven_front", tag="wk_raw00", align_bytes=64)
+        woven_1 = [woven_front[:, PACK * STARTS[c] : PACK * (STARTS[c] + WIDTHS[c])] for c in range(PAIRED)]
+        weave_pair(woven_front, 1, 0, front)
         deal_wk(nc.scalar.copy, 0, 1)
-        for c in range(PAIRED):
-            weave_pair(woven_1[c], 1, 0, cols_of(c))
-        quantize_wk(0)
         gather_front(1, 2, front)
+        gather_rest(2)
+        quantize_wk(0)
         deal_wk(nc.scalar.copy, 1, 0)
 
         value_banks = {0: take(0), 1: take(2, 3), 2: take(6, 7)}
         key_banks = {0: take(1), 1: take(4, 5)}
-        for c in range(EARLY):
+        for c in range(PAIRED):
             value_pass(value_banks[c], c, 0)
+        for c in range(EARLY):
             key_pass(key_banks[c], c, 0)
-        value_pass(value_banks[2], 2, 0)
 
         def close_value(c):
             quantize_xg(1, woven_1[c][:], cols_of(c))
@@ -389,7 +390,6 @@ def tile_list_hwaytanhP_kernel(
         for c in range(EARLY):
             key_pass(key_banks[c], c, 1)
         close_value(2)
-        gather_rest(2)
         gather_rest(3)
         diff = {0: difference(0)}
         nc.vector.tensor_copy(

@@ -342,11 +342,11 @@ def tile_list_hwaytanhP_kernel(
 
         whole = slice(0, J)
         front = slice(0, FRONT)
-        gather_front(0, 0, whole)
-        nc.vector.tensor_copy(
+        nc.scalar.copy(
             out=wv_codes[:].bitcast(U16).rearrange("p a (t m) -> p a t m", t=PACK),
             in_=wv_raw[:].bitcast(U16).rearrange("p a (m t) -> p a t m", t=PACK),
         )
+        gather_front(0, 0, whole)
         gather_front(0, 1, whole)
         weave_pair(woven_0, 0, 0, whole)
         gather_front(0, 2, whole)

@@ -65,7 +65,7 @@ def tile_list_hwaytanhP_kernel(
         compact_turned = held("compact_turned", [P, J // GROUP], F32)
         repeated = keep.tile([P, J], F32, name="repeated", tag="picked1", align_bytes=64)
         bias = held("bias", [P, PACK], F32)
-        half_bias = held("half_bias", [P, PACK], F32)
+        half_bias = {c: held("half_bias%d" % c, [P, PACK], F32) for c in range(2, CHUNKS)}
         planes = [[in_place_of(a, i, "plane", [P, T], F32) for i in range(PACK)] for a in range(PASSES)]
         wvs_raw = held("wvs_raw", [P, N], U8)
         wvs_dealt = held("wvs_dealt", [P, N], U8)
@@ -206,7 +206,7 @@ def tile_list_hwaytanhP_kernel(
                     out=result[:, t * w : (t + 1) * w],
                     in_=bank[:, lo : lo + w],
                     func=TANH,
-                    bias=half_bias[:, t : t + 1],
+                    bias=half_bias[max(c, 2)][:, t : t + 1],
                     scale=0.5,
                 )
             return result
@@ -285,8 +285,8 @@ def tile_list_hwaytanhP_kernel(
             nc.sync.dma_start(out=rows[:, :, cols_of(c)], in_=result)
             return result
 
-        def weave_out(copy, c, y, name, bufs):
-            result = work.tile([P, WIDTHS[c] * PACK], BF16, name=name, align_bytes=64, bufs=bufs)
+        def weave_out(copy, c, y, tag):
+            result = keep.tile([P, WIDTHS[c] * PACK], BF16, name="woven_out", tag=tag, align_bytes=64)
             copy(
                 out=result[:].rearrange("p (c e t) -> p c t e", e=4, t=PACK),
                 in_=y.rearrange("p t (c e) -> p c t e", e=4),
@@ -352,7 +352,8 @@ def tile_list_hwaytanhP_kernel(
         gather_front(0, 2, whole)
         gather_front(0, 3, whole)
         weave_pair(woven_0, 0, 1, whole)
-        nc.scalar.mul(half_bias[:], bias[:], 0.5)
+        for c in range(2, CHUNKS):
+            nc.scalar.mul(half_bias[c][:], bias[:], 0.5)
         deal_wk(nc.scalar.copy, 0, 0)
         for i in range(2):
             gather_front(1, i, front)
@@ -418,6 +419,11 @@ def tile_list_hwaytanhP_kernel(
         res_turned[3] = negate(res_banks, 3)
         key_products(take(6, 7), 3)
         tanh_ke[2] = key_tanh(key_banks[2], 2)
+        y_all = keep.tile([P, PACK * J], F32, name="y_all", tag="picked0", align_bytes=64)
+        twice = {c: gated(c) for c in range(2)}
+        woven_out = {0: weave_out(nc.scalar.copy, 0, finish(0, twice[0]), "half_bias2")}
+        diff[2] = difference(2)
+        y = finish(1, twice[1])
         value_banks[4] = turned_value(take(4), 4)
         res_banks = turn_res(take(5), 4)
         diff[3] = take(0, 2)
@@ -426,6 +432,7 @@ def tile_list_hwaytanhP_kernel(
         key_products(take(3), 4)
         add_turned(diff[3], tanh_ve[3], False)
         tanh_ke[3] = key_tanh(key_banks[3], 3)
+        woven_out[1] = weave_out(nc.scalar.copy, 1, y, "half_bias3")
         res_turned[4] = negate(res_banks, 4)
         diff[4] = take(1)
         add_turned(diff[4], res_turned[4], True)
@@ -433,21 +440,16 @@ def tile_list_hwaytanhP_kernel(
         add_turned(diff[4], tanh_ve[4], False)
         tanh_ke[4] = key_tanh(key_banks[4], 4)
 
-        woven_out = {}
-        y_all = keep.tile([P, PACK * J], F32, name="y_all", tag="picked0", align_bytes=64)
-        for c in range(CHUNKS):
-            twice = gated(c)
-            if c == 1:
-                diff[c + 1] = difference(c + 1)
-            if c >= 2:
-                quantize_out(c - 2)
-                store_codes(cols_of(c - 2))
-            y = finish(c, twice)
+        for c in range(2, CHUNKS):
+            twice[c] = gated(c)
+            quantize_out(c - 2)
+            store_codes(cols_of(c - 2))
+            y = finish(c, twice[c])
             if c < LAST:
-                woven_out[c] = weave_out(nc.scalar.copy, c, y, "woven_out", LAST)
+                woven_out[c] = weave_out(nc.scalar.copy, c, y, ("half_bias4", "woven_out3")[c - 2])
+        woven_out[LAST] = weave_out(nc.vector.tensor_copy, LAST, y, "woven_out4")
         quantize_out(LAST - 1)
         store_codes(cols_of(LAST - 1))
-        woven_out[LAST] = weave_out(nc.vector.tensor_copy, LAST, y, "woven_last", 1)
         quantize_out(LAST)
         store_codes(cols_of(LAST))
 

@@ -29,6 +29,7 @@ LIST = 16
 GROUP = P // HEADS
 SQUARE = 32
 QUADRANTS = 4
+SPREAD = 4
 
 WIDTHS = [128, 256, 256, 256, 128]
 STARTS = [sum(WIDTHS[:c]) for c in range(len(WIDTHS))]
@@ -40,6 +41,7 @@ FRONT = STARTS[PAIRED]
 REST = J - FRONT
 PLACE = [0, 1, 2, 3, 4, 5, 1, 2]
 TURNED_PLACE = {3: 0, 4: 3}
+BIAS_TILES = range(2, CHUNKS)
 
 
 def tile_list_hwaytanhP_kernel(
@@ -65,19 +67,19 @@ def tile_list_hwaytanhP_kernel(
         compact_turned = held("compact_turned", [P, J // GROUP], F32)
         repeated = keep.tile([P, J], F32, name="repeated", tag="picked1", align_bytes=64)
         bias = held("bias", [P, PACK], F32)
-        half_bias = {c: held("half_bias%d" % c, [P, PACK], F32) for c in range(2, CHUNKS)}
+        half_bias = {c: held("half_bias%d" % c, [P, PACK], F32) for c in BIAS_TILES}
         planes = [[in_place_of(a, i, "plane", [P, T], F32) for i in range(PACK)] for a in range(PASSES)]
         wvs_raw = held("wvs_raw", [P, N], U8)
         wvs_dealt = held("wvs_dealt", [P, N], U8)
         wv_scale = held("wv_scale", [P, PASSES, N], U8)
         picked = [held("picked0", [P, PACK * J], F32), held("picked1", [P, PACK * FRONT], F32)]
-        picked_rest = held("picked_rest", [P, 3 * REST + N * PACK // 2], F32)
+        picked_rest = held("picked_rest", [P, (PACK - 1) * REST + N * PACK // 2], F32)
         xg_codes = {1: held("xg_codes1", [P, J], U32)}
         woven_0 = held("woven_0", [P, J * PACK], BF16)
         woven_rest = held("woven_rest", [P, REST * PACK], BF16)
         xg_scale = [held("xg_scale%d" % a, [P, J], U8) for a in range(PASSES)]
         wk_raw = [[held("wk_raw%d%d" % (a, h), [P, PACK, N // 2], F32) for h in range(2)] for a in range(PASSES)]
-        wk_bf = [held("wk_bf0", [P, N * PACK], BF16)[:], picked_rest[:, 3 * REST :].bitcast(BF16)]
+        wk_bf = [held("wk_bf0", [P, N * PACK], BF16)[:], picked_rest[:, (PACK - 1) * REST :].bitcast(BF16)]
         wk_codes = [held("wk_codes%d" % a, [P, N], U32) for a in range(PASSES)]
         wk_scale = [held("wk_scale%d" % a, [P, N], U8) for a in range(PASSES)]
         carried = [held("carried%d" % c, [P, PACK, WIDTHS[c]], F32) for c in range(CHUNKS)]
@@ -106,12 +108,12 @@ def tile_list_hwaytanhP_kernel(
                 nc.vector.transpose(compact_turned[:, cols], compact[:, cols])
             runs = squares * SQUARE // GROUP
             by_c = compact_turned[:].rearrange("p (k c) -> p c k", c=GROUP)
-            for h in range(4):
-                part = slice(h * J // 4, (h + 1) * J // 4)
-                source = by_c[:, h * GROUP // 4 : (h + 1) * GROUP // 4, :]
+            for h in range(SPREAD):
+                part = slice(h * J // SPREAD, (h + 1) * J // SPREAD)
+                source = by_c[:, h * GROUP // SPREAD : (h + 1) * GROUP // SPREAD, :]
                 nc.scalar.copy(
                     out=repeated[:, part].rearrange("p (c k r) -> p c k r", k=runs, r=GROUP),
-                    in_=source.unsqueeze(3).to_broadcast([P, GROUP // 4, runs, GROUP]),
+                    in_=source.unsqueeze(3).to_broadcast([P, GROUP // SPREAD, runs, GROUP]),
                 )
                 nc.vector.transpose(weights[:, part], repeated[:, part])
 
@@ -206,7 +208,7 @@ def tile_list_hwaytanhP_kernel(
                     out=result[:, t * w : (t + 1) * w],
                     in_=bank[:, lo : lo + w],
                     func=TANH,
-                    bias=half_bias[max(c, 2)][:, t : t + 1],
+                    bias=half_bias[max(c, BIAS_TILES[0])][:, t : t + 1],
                     scale=0.5,
                 )
             return result
@@ -277,20 +279,23 @@ def tile_list_hwaytanhP_kernel(
                 nc.vector.scalar_tensor_tensor(result[:], tanh_ke[c][:], 1.0, diff[c][:], ALU.add, ALU.mult)
             return result
 
-        def finish(c, twice):
+        def finish(c):
             run = y_all[:, PACK * STARTS[c] : PACK * (STARTS[c] + WIDTHS[c])]
-            nc.vector.scalar_tensor_tensor(run, twice[:], 0.5, flat(carried[c]), ALU.mult, ALU.add)
+            nc.vector.scalar_tensor_tensor(run, twice[c][:], 0.5, flat(carried[c]), ALU.mult, ALU.add)
             result = run.rearrange("p (t j) -> p t j", t=PACK)
             rows = out_0.rearrange("(p t) j -> p t j", t=PACK)
             nc.sync.dma_start(out=rows[:, :, cols_of(c)], in_=result)
             return result
 
-        def weave_out(copy, c, y, tag):
-            result = keep.tile([P, WIDTHS[c] * PACK], BF16, name="woven_out", tag=tag, align_bytes=64)
+        def weave_rows(copy, dst, rows):
             copy(
-                out=result[:].rearrange("p (c e t) -> p c t e", e=4, t=PACK),
-                in_=y.rearrange("p t (c e) -> p c t e", e=4),
+                out=dst.rearrange("p (c e t) -> p c t e", e=4, t=PACK),
+                in_=rows.rearrange("p t (c e) -> p c t e", e=4),
             )
+
+        def weave_out(copy, c, tag):
+            result = keep.tile([P, WIDTHS[c] * PACK], BF16, name="woven_out", tag=tag, align_bytes=64)
+            weave_rows(copy, result[:], y[c])
             return result
 
         def quantize_out(c):
@@ -314,8 +319,9 @@ def tile_list_hwaytanhP_kernel(
         nc.scalar.dma_start(out=compact[:], in_=first_rows.rearrange("g (c e) -> g c e", c=GROUP))
         nc.sync.dma_start(out=wvs_raw[:32, :].bitcast(I32), in_=wv_scales.rearrange("a r n -> r a n").bitcast(I32))
         load_plane(0, 0)
+        load_plane(0, 1)
         nc.sync.dma_start(out=wv_raw[:].bitcast(I32), in_=wv_words.rearrange("a p b -> p a b").bitcast(I32))
-        for i in range(1, PACK):
+        for i in range(2, PACK):
             load_plane(0, i)
         load_plane(1, 0)
         load_plane(1, 1)
@@ -352,7 +358,7 @@ def tile_list_hwaytanhP_kernel(
         gather_front(0, 2, whole)
         gather_front(0, 3, whole)
         weave_pair(woven_0, 0, 1, whole)
-        for c in range(2, CHUNKS):
+        for c in BIAS_TILES:
             nc.scalar.mul(half_bias[c][:], bias[:], 0.5)
         deal_wk(nc.scalar.copy, 0, 0)
         for i in range(2):
@@ -393,9 +399,8 @@ def tile_list_hwaytanhP_kernel(
         close_value(2)
         gather_rest(3)
         diff = {0: difference(0)}
-        nc.vector.tensor_copy(
-            out=woven_rest[:].rearrange("p (c e i) -> p c i e", e=4, i=PACK),
-            in_=picked_rest[:, : PACK * REST].rearrange("p (i c e) -> p c i e", e=4, i=PACK),
+        weave_rows(
+            nc.vector.tensor_copy, woven_rest[:], picked_rest[:, : PACK * REST].rearrange("p (i j) -> p i j", i=PACK)
         )
         diff[1] = difference(1)
         for c in range(PAIRED, CHUNKS):
@@ -421,9 +426,10 @@ def tile_list_hwaytanhP_kernel(
         tanh_ke[2] = key_tanh(key_banks[2], 2)
         y_all = keep.tile([P, PACK * J], F32, name="y_all", tag="picked0", align_bytes=64)
         twice = {c: gated(c) for c in range(2)}
-        woven_out = {0: weave_out(nc.scalar.copy, 0, finish(0, twice[0]), "half_bias2")}
+        y = {0: finish(0)}
+        woven_out = {0: weave_out(nc.scalar.copy, 0, "half_bias2")}
         diff[2] = difference(2)
-        y = finish(1, twice[1])
+        y[1] = finish(1)
         value_banks[4] = turned_value(take(4), 4)
         res_banks = turn_res(take(5), 4)
         diff[3] = take(0, 2)
@@ -432,7 +438,7 @@ def tile_list_hwaytanhP_kernel(
         key_products(take(3), 4)
         add_turned(diff[3], tanh_ve[3], False)
         tanh_ke[3] = key_tanh(key_banks[3], 3)
-        woven_out[1] = weave_out(nc.scalar.copy, 1, y, "half_bias3")
+        woven_out[1] = weave_out(nc.scalar.copy, 1, "half_bias3")
         res_turned[4] = negate(res_banks, 4)
         diff[4] = take(1)
         add_turned(diff[4], res_turned[4], True)
@@ -440,18 +446,23 @@ def tile_list_hwaytanhP_kernel(
         add_turned(diff[4], tanh_ve[4], False)
         tanh_ke[4] = key_tanh(key_banks[4], 4)
 
-        for c in range(2, CHUNKS):
+        def close_chunk(c):
             twice[c] = gated(c)
             quantize_out(c - 2)
             store_codes(cols_of(c - 2))
-            y = finish(c, twice[c])
-            if c < LAST:
-                woven_out[c] = weave_out(nc.scalar.copy, c, y, ("half_bias4", "woven_out3")[c - 2])
-        woven_out[LAST] = weave_out(nc.vector.tensor_copy, LAST, y, "woven_out4")
+            y[c] = finish(c)
+
+        close_chunk(2)
+        woven_out[2] = weave_out(nc.scalar.copy, 2, "half_bias4")
+        close_chunk(3)
+        woven_out[3] = held("woven_out3", [P, WIDTHS[3] * PACK], BF16)
+        weave_rows(nc.scalar.copy, woven_out[3][:, : PACK * P], y[3][:, :, :P])
+        close_chunk(LAST)
+        weave_rows(nc.vector.tensor_copy, woven_out[3][:, PACK * P :], y[3][:, :, P:])
+        woven_out[LAST] = weave_out(nc.vector.tensor_copy, LAST, "woven_out4")
         quantize_out(LAST - 1)
-        store_codes(cols_of(LAST - 1))
         quantize_out(LAST)
-        store_codes(cols_of(LAST))
+        store_codes(slice(STARTS[LAST - 1], J))
 
         for q in range(QUADRANTS):
             queue = nc.sync if q % 2 == 0 else nc.scalar

from contextlib import ExitStack

import concourse.mybir as mybir
from concourse.masks import make_identity

K, N, T, J = 1024, 512, 2048, 1024
HEADS = 8
FLOPS = 2 * 2 * K * N * J
BYTES = 4 * (K * T + HEADS * J + K * N + N + 2 * N * J) + K * N // 2 + K * N // 32 + N * J + N * J // 32 + 2 * HEADS * J

F32 = mybir.dt.float32
BF16 = mybir.dt.bfloat16
I32 = mybir.dt.int32
U32 = mybir.dt.uint32
U16 = mybir.dt.uint16
U8 = mybir.dt.uint8
FP8X4 = mybir.dt.float8_e4m3fn_x4
FP4X4 = mybir.dt.float4_e2m1fn_x4
ALU = mybir.AluOpType
TANH = mybir.ActivationFunctionType.Tanh
COPY = mybir.ActivationFunctionType.Copy

P = 128
PACK = 4
K_PASS = P * PACK
PASSES = K // K_PASS
BANK = 512
LIST = 16
GROUP = P // HEADS
SQUARE = 32
QUADRANTS = 4
SPREAD = 4

WIDTHS = [128, 256, 256, 256, 128]
STARTS = [sum(WIDTHS[:c]) for c in range(len(WIDTHS))]
CHUNKS = len(WIDTHS)
LAST = CHUNKS - 1
EARLY = 2
PAIRED = 3
FRONT = STARTS[PAIRED]
REST = J - FRONT
PLACE = [0, 1, 2, 3, 4, 5, 1, 2]
TURNED_PLACE = {3: 0, 4: 3}
BIAS_TILES = range(2, CHUNKS)


def tile_list_hwaytanhP_kernel(
    tc, xT, wgt, wk, wv_words, wv_scales, bg, res, offs, out_0, out_1, out_2
):
    nc = tc.nc
    with ExitStack() as ctx:
        keep = ctx.enter_context(tc.tile_pool(name="keep", bufs=1))
        work = ctx.enter_context(tc.tile_pool(name="work", bufs=2))
        psum = ctx.enter_context(tc.psum_pool(name="psum", bufs=1))

        def held(name, shape, dtype):
            return keep.tile(shape, dtype, name=name, align_bytes=64)

        def in_place_of(a, i, name, shape, dtype):
            return keep.tile(shape, dtype, name=name, tag="place%d" % PLACE[PACK * a + i], align_bytes=64)

        offsets = held("offsets", [P, J // LIST], U16)
        wv_raw = held("wv_raw", [P, PASSES, 2 * N], U8)
        wv_codes = held("wv_codes", [P, PASSES, 2 * N], U8)
        weights = held("weights", [P, J], F32)
        compact = held("compact", [P, J // GROUP], F32)
        compact_turned = held("compact_turned", [P, J // GROUP], F32)
        repeated = keep.tile([P, J], F32, name="repeated", tag="picked1", align_bytes=64)
        bias = held("bias", [P, PACK], F32)
        half_bias = {c: held("half_bias%d" % c, [P, PACK], F32) for c in BIAS_TILES}
        planes = [[in_place_of(a, i, "plane", [P, T], F32) for i in range(PACK)] for a in range(PASSES)]
        wvs_raw = held("wvs_raw", [P, N], U8)
        wvs_dealt = held("wvs_dealt", [P, N], U8)
        wv_scale = held("wv_scale", [P, PASSES, N], U8)
        picked = [held("picked0", [P, PACK * J], F32), held("picked1", [P, PACK * FRONT], F32)]
        picked_rest = held("picked_rest", [P, (PACK - 1) * REST + N * PACK // 2], F32)
        xg_codes = {1: held("xg_codes1", [P, J], U32)}
        woven_0 = held("woven_0", [P, J * PACK], BF16)
        woven_rest = held("woven_rest", [P, REST * PACK], BF16)
        xg_scale = [held("xg_scale%d" % a, [P, J], U8) for a in range(PASSES)]
        wk_raw = [[held("wk_raw%d%d" % (a, h), [P, PACK, N // 2], F32) for h in range(2)] for a in range(PASSES)]
        wk_bf = [held("wk_bf0", [P, N * PACK], BF16)[:], picked_rest[:, (PACK - 1) * REST :].bitcast(BF16)]
        wk_codes = [held("wk_codes%d" % a, [P, N], U32) for a in range(PASSES)]
        wk_scale = [held("wk_scale%d" % a, [P, N], U8) for a in range(PASSES)]
        carried = [held("carried%d" % c, [P, PACK, WIDTHS[c]], F32) for c in range(CHUNKS)]
        out_codes = held("out_codes", [P, J], U32)
        out_scale = held("out_scale", [P, J], U8)

        def cols_of(c):
            return slice(STARTS[c], STARTS[c] + WIDTHS[c])

        def load_plane(a, i):
            rows = xT[a * K_PASS : (a + 1) * K_PASS, :].rearrange("(p i) t -> p i t", i=PACK)
            nc.sync.dma_start(out=planes[a][i][:], in_=rows[:, i, :])

        def load_wk(a, h):
            rows = wk[a * K_PASS : (a + 1) * K_PASS, :].rearrange("(p i) n -> p i n", i=PACK)
            nc.sync.dma_start(out=wk_raw[a][h][:], in_=rows[:, :, h * (N // 2) : (h + 1) * (N // 2)])

        def load_res(c):
            rows = res.rearrange("(p t) j -> p t j", t=PACK)
            nc.sync.dma_start(out=carried[c][:], in_=rows[:, :, cols_of(c)])

        def spread_weights():
            squares = J // GROUP // SQUARE
            for b in range(squares):
                cols = slice(SQUARE * b, SQUARE * (b + 1))
                nc.vector.transpose(compact_turned[:, cols], compact[:, cols])
            runs = squares * SQUARE // GROUP
            by_c = compact_turned[:].rearrange("p (k c) -> p c k", c=GROUP)
            for h in range(SPREAD):
                part = slice(h * J // SPREAD, (h + 1) * J // SPREAD)
                source = by_c[:, h * GROUP // SPREAD : (h + 1) * GROUP // SPREAD, :]
                nc.scalar.copy(
                    out=repeated[:, part].rearrange("p (c k r) -> p c k r", k=runs, r=GROUP),
                    in_=source.unsqueeze(3).to_broadcast([P, GROUP // SPREAD, runs, GROUP]),
                )
                nc.vector.transpose(weights[:, part], repeated[:, part])

        def gather(dst, a, i, cols):
            nc.vector.tensor_tensor(
                dst,
                planes[a][i][:].indirect(offsets[:, cols.start // LIST : cols.stop // LIST]),
                weights[:, cols],
                ALU.mult,
            )

        def gather_front(a, i, cols):
            width = (J, FRONT)[a]
            gather(picked[a][:, i * width + cols.start : i * width + cols.stop], a, i, cols)

        def gather_rest(i):
            gather(picked_rest[:, i * REST : (i + 1) * REST], 1, i, slice(FRONT, J))

        def weave_pair(dst, a, u, cols):
            rows = picked[a][:].rearrange("p (i j) -> p i j", i=PACK)
            nc.scalar.copy(
                out=dst[:].rearrange("p (j i) -> p j i", i=PACK)[:, :, 2 * u : 2 * u + 2],
                in_=rows[:, 2 * u : 2 * u + 2, cols].rearrange("p i j -> p j i"),
            )

        def quantize_xg(a, woven, cols):
            nc.vector.quantize_mx(out=xg_codes[a][:, cols].bitcast(FP8X4), scales=xg_scale[a][:, cols], in_=woven)

        def deal_wk(copy, a, h):
            copy(
                out=wk_bf[a].rearrange("p (t m i) -> p m i t", t=PACK, i=PACK)[:, h * (P // 2) : (h + 1) * (P // 2)],
                in_=wk_raw[a][h][:].rearrange("p i (m t) -> p m i t", t=PACK),
            )

        def quantize_wk(a):
            nc.vector.quantize_mx(
                out=wk_codes[a][:].bitcast(FP8X4),
                scales=wk_scale[a][:],
                in_=wk_bf[a],
            )

        def take(*numbers):
            return [psum.tile([P, BANK], F32, name="bank%d" % u) for u in numbers]

        def place(banks, c, t):
            per_bank = BANK // WIDTHS[c]
            lo = (t % per_bank) * WIDTHS[c]
            return banks[t // per_bank], lo, t % per_bank == 0, t % per_bank == per_bank - 1

        def value_pass(banks, c, a):
            pieces = WIDTHS[c] // P
            for t in range(PACK):
                bank, lo, opens, closes = place(banks, c, t)
                for s in range(pieces):
                    cols = slice(STARTS[c] + s * P, STARTS[c] + (s + 1) * P)
                    nc.tensor.matmul_mx(
                        out=bank[:, lo + s * P : lo + (s + 1) * P],
                        lhsT=wv_codes[:, a, 2 * P * t : 2 * P * (t + 1)].bitcast(FP4X4),
                        lhsT_scale=wv_scale[:, a, P * t : P * (t + 1)],
                        rhs=xg_codes[a][:, cols].bitcast(FP8X4),
                        rhs_scale=xg_scale[a][:, cols],
                        start=(a == 0 and opens and s == 0),
                        stop=(a == PASSES - 1 and closes and s == pieces - 1),
                    )

        def key_pass(banks, c, a):
            cols = cols_of(c)
            for t in range(PACK):
                bank, lo, opens, closes = place(banks, c, t)
                nc.tensor.matmul_mx(
                    out=bank[:, lo : lo + WIDTHS[c]],
                    lhsT=wk_codes[a][:, P * t : P * (t + 1)].bitcast(FP8X4),
                    lhsT_scale=wk_scale[a][:, P * t : P * (t + 1)],
                    rhs=xg_codes[a][:, cols].bitcast(FP8X4),
                    rhs_scale=xg_scale[a][:, cols],
                    start=(a == 0 and opens),
                    stop=(a == PASSES - 1 and closes),
                )

        def value_tanh(banks, c):
            result = held("tanh_ve%d" % c, [P, PACK * WIDTHS[c]], F32)
            for u, bank in enumerate(banks):
                nc.scalar.activation(out=result[:, u * BANK : (u + 1) * BANK], in_=bank[:], func=TANH)
            return result

        def key_tanh(banks, c):
            w = WIDTHS[c]
            result = held("tanh_ke%d" % c, [P, PACK * w], F32)
            for t in range(PACK):
                bank, lo, opens, closes = place(banks, c, t)
                nc.scalar.activation(
                    out=result[:, t * w : (t + 1) * w],
                    in_=bank[:, lo : lo + w],
                    func=TANH,
                    bias=half_bias[max(c, BIAS_TILES[0])][:, t : t + 1],
                    scale=0.5,
                )
            return result

        def flat(tile):
            return tile[:].rearrange("p t j -> p (t j)")

        def difference(c):
            result = work.tile([P, PACK * WIDTHS[c]], F32, name="diff", bufs=3)
            nc.vector.tensor_tensor(result[:], tanh_ve[c][:], flat(carried[c]), ALU.subtract)
            return result

        def turn_res(banks, c):
            for s, bank in enumerate(banks):
                for t in range(PACK):
                    nc.tensor.transpose(
                        bank[:, P * t : P * (t + 1)], carried[c][:, t, P * s : P * (s + 1)], identity[:]
                    )
            return banks

        def negate(banks, c):
            result = in_place_of(0, TURNED_PLACE[c], "res_turned", [P, PACK * WIDTHS[c]], F32)
            for s, bank in enumerate(banks):
                nc.scalar.activation(out=result[:, BANK * s : BANK * (s + 1)], in_=bank[:], func=COPY, scale=-1.0)
            return result

        def turned_value(banks, c):
            for s, bank in enumerate(banks):
                cols = slice(STARTS[c] + s * P, STARTS[c] + (s + 1) * P)
                for a in range(PASSES):
                    nc.tensor.matmul_mx(
                        out=bank[:],
                        lhsT=xg_codes[a][:, cols].bitcast(FP8X4),
                        lhsT_scale=xg_scale[a][:, cols],
                        rhs=wv_codes[:, a, :].bitcast(FP4X4),
                        rhs_scale=wv_scale[:, a, :],
                        start=(a == 0),
                        stop=(a == PASSES - 1),
                    )
            return banks

        def add_turned(banks, source, first):
            for s, bank in enumerate(banks):
                for t in range(PACK):
                    nc.tensor.matmul(
                        bank[:, P * t : P * (t + 1)],
                        source[:, BANK * s + P * t : BANK * s + P * (t + 1)],
                        identity[:],
                        start=(first and t == 0),
                        stop=(not first and t == PACK - 1),
                        is_transpose=True,
                    )

        def gated(c):
            result = work.tile([P, PACK * WIDTHS[c]], F32, name="twice")
            if c in TURNED_PLACE:
                for s, bank in enumerate(diff[c]):
                    cols = slice(s * P, (s + 1) * P)
                    nc.vector.scalar_tensor_tensor(
                        result[:].rearrange("p (t j) -> p t j", t=PACK)[:, :, cols],
                        tanh_ke[c][:].rearrange("p (t j) -> p t j", t=PACK)[:, :, cols],
                        1.0,
                        bank[:].rearrange("p (t j) -> p t j", t=PACK),
                        ALU.add,
                        ALU.mult,
                    )
            else:
                nc.vector.scalar_tensor_tensor(result[:], tanh_ke[c][:], 1.0, diff[c][:], ALU.add, ALU.mult)
            return result

        def finish(c):
            run = y_all[:, PACK * STARTS[c] : PACK * (STARTS[c] + WIDTHS[c])]
            nc.vector.scalar_tensor_tensor(run, twice[c][:], 0.5, flat(carried[c]), ALU.mult, ALU.add)
            result = run.rearrange("p (t j) -> p t j", t=PACK)
            rows = out_0.rearrange("(p t) j -> p t j", t=PACK)
            nc.sync.dma_start(out=rows[:, :, cols_of(c)], in_=result)
            return result

        def weave_rows(copy, dst, rows):
            copy(
                out=dst.rearrange("p (c e t) -> p c t e", e=4, t=PACK),
                in_=rows.rearrange("p t (c e) -> p c t e", e=4),
            )

        def weave_out(copy, c, tag):
            result = keep.tile([P, WIDTHS[c] * PACK], BF16, name="woven_out", tag=tag, align_bytes=64)
            weave_rows(copy, result[:], y[c])
            return result

        def quantize_out(c):
            cols = cols_of(c)
            nc.vector.quantize_mx(
                out=out_codes[:, cols].bitcast(FP8X4), scales=out_scale[:, cols], in_=woven_out[c][:]
            )

        def store_codes(cols):
            words = out_1[0].rearrange("p j t -> p (j t)").bitcast(I32)
            nc.sync.dma_start(out=words[:, cols], in_=out_codes[:, cols].bitcast(I32))

        nc.gpsimd.memset(wvs_raw[32:64, :].bitcast(I32), 0)
        nc.gpsimd.memset(wvs_raw[64:, :].bitcast(I32), 0)
        nc.gpsimd.memset(wv_scale[:].rearrange("p a n -> p (a n)").bitcast(I32), 0)
        identity = held("identity", [P, P], F32)
        make_identity(nc, identity[:])

        nc.sync.dma_start(offsets[:], offs)
        first_rows = wgt.rearrange("(g r) j -> g r j", r=GROUP)[:, 0, :]
        nc.scalar.dma_start(out=compact[:], in_=first_rows.rearrange("g (c e) -> g c e", c=GROUP))
        nc.sync.dma_start(out=wvs_raw[:32, :].bitcast(I32), in_=wv_scales.rearrange("a r n -> r a n").bitcast(I32))
        load_plane(0, 0)
        load_plane(0, 1)
        nc.sync.dma_start(out=wv_raw[:].bitcast(I32), in_=wv_words.rearrange("a p b -> p a b").bitcast(I32))
        for i in range(2, PACK):
            load_plane(0, i)
        load_plane(1, 0)
        load_plane(1, 1)
        nc.sync.dma_start(out=bias[:], in_=bg.rearrange("(p t) -> p t", t=PACK))
        load_wk(0, 0)
        load_plane(1, 2)
        load_wk(0, 1)
        load_wk(1, 0)
        load_plane(1, 3)
        load_wk(1, 1)
        for c in (0, 1, 3, 4, 2):
            load_res(c)

        spread_weights()
        nc.vector.tensor_copy(
            out=wvs_dealt[:].rearrange("p (t m) -> p t m", t=PACK),
            in_=wvs_raw[:].rearrange("p (m t) -> p t m", t=PACK),
        )
        for q in range(QUADRANTS):
            nc.gpsimd.dma_start(
                out=wv_scale[32 * q : 32 * q + 4, :, :].bitcast(I32),
                in_=wvs_dealt[8 * q : 8 * q + 8, :].bitcast(I32),
            )

        whole = slice(0, J)
        front = slice(0, FRONT)
        nc.scalar.copy(
            out=wv_codes[:].bitcast(U16).rearrange("p a (t m) -> p a t m", t=PACK),
            in_=wv_raw[:].bitcast(U16).rearrange("p a (m t) -> p a t m", t=PACK),
        )
        gather_front(0, 0, whole)
        gather_front(0, 1, whole)
        weave_pair(woven_0, 0, 0, whole)
        gather_front(0, 2, whole)
        gather_front(0, 3, whole)
        weave_pair(woven_0, 0, 1, whole)
        for c in BIAS_TILES:
            nc.scalar.mul(half_bias[c][:], bias[:], 0.5)
        deal_wk(nc.scalar.copy, 0, 0)
        for i in range(2):
            gather_front(1, i, front)
            gather_rest(i)
        xg_codes[0] = in_place_of(1, 1, "xg_codes0", [P, J], U32)
        quantize_xg(0, woven_0[:], whole)
        woven_front = keep.tile([P, FRONT * PACK], BF16, name="woven_front", tag="wk_raw00", align_bytes=64)
        woven_1 = [woven_front[:, PACK * STARTS[c] : PACK * (STARTS[c] + WIDTHS[c])] for c in range(PAIRED)]
        weave_pair(woven_front, 1, 0, front)
        deal_wk(nc.scalar.copy, 0, 1)
        gather_front(1, 2, front)
        gather_rest(2)
        quantize_wk(0)
        deal_wk(nc.scalar.copy, 1, 0)

        value_banks = {0: take(0), 1: take(2, 3), 2: take(6, 7)}
        key_banks = {0: take(1), 1: take(4, 5)}
        for c in range(PAIRED):
            value_pass(value_banks[c], c, 0)
        for c in range(EARLY):
            key_pass(key_banks[c], c, 0)

        def close_value(c):
            quantize_xg(1, woven_1[c][:], cols_of(c))
            value_pass(value_banks[c], c, 1)

        for c in range(PAIRED):
            gather_front(1, 3, cols_of(c))
            weave_pair(woven_1[c], 1, 1, cols_of(c))
        for c in range(EARLY):
            close_value(c)
        deal_wk(nc.vector.tensor_copy, 1, 1)
        tanh_ve = {c: value_tanh(value_banks[c], c) for c in range(EARLY)}
        quantize_wk(1)
        for c in range(EARLY):
            key_pass(key_banks[c], c, 1)
        close_value(2)
        gather_rest(3)
        diff = {0: difference(0)}
        weave_rows(
            nc.vector.tensor_copy, woven_rest[:], picked_rest[:, : PACK * REST].rearrange("p (i j) -> p i j", i=PACK)
        )
        diff[1] = difference(1)
        for c in range(PAIRED, CHUNKS):
            lo = PACK * (STARTS[c] - FRONT)
            quantize_xg(1, woven_rest[:, lo : lo + PACK * WIDTHS[c]], cols_of(c))

        tanh_ke = {}
        res_turned = {}

        def key_products(banks, c):
            key_banks[c] = banks
            key_pass(banks, c, 0)
            key_pass(banks, c, 1)

        tanh_ke[0] = key_tanh(key_banks[0], 0)
        key_products(take(0, 2), 2)
        tanh_ke[1] = key_tanh(key_banks[1], 1)
        tanh_ve[2] = value_tanh(value_banks[2], 2)
        res_banks = turn_res(take(4, 5), 3)
        value_banks[3] = turned_value(take(3, 1), 3)
        res_turned[3] = negate(res_banks, 3)
        key_products(take(6, 7), 3)
        tanh_ke[2] = key_tanh(key_banks[2], 2)
        y_all = keep.tile([P, PACK * J], F32, name="y_all", tag="picked0", align_bytes=64)
        twice = {c: gated(c) for c in range(2)}
        y = {0: finish(0)}
        woven_out = {0: weave_out(nc.scalar.copy, 0, "half_bias2")}
        diff[2] = difference(2)
        y[1] = finish(1)
        value_banks[4] = turned_value(take(4), 4)
        res_banks = turn_res(take(5), 4)
        diff[3] = take(0, 2)
        add_turned(diff[3], res_turned[3], True)
        tanh_ve[3] = value_tanh(value_banks[3], 3)
        key_products(take(3), 4)
        add_turned(diff[3], tanh_ve[3], False)
        tanh_ke[3] = key_tanh(key_banks[3], 3)
        woven_out[1] = weave_out(nc.scalar.copy, 1, "half_bias3")
        res_turned[4] = negate(res_banks, 4)
        diff[4] = take(1)
        add_turned(diff[4], res_turned[4], True)
        tanh_ve[4] = value_tanh(value_banks[4], 4)
        add_turned(diff[4], tanh_ve[4], False)
        tanh_ke[4] = key_tanh(key_banks[4], 4)

        def close_chunk(c):
            twice[c] = gated(c)
            quantize_out(c - 2)
            store_codes(cols_of(c - 2))
            y[c] = finish(c)

        close_chunk(2)
        woven_out[2] = weave_out(nc.scalar.copy, 2, "half_bias4")
        close_chunk(3)
        woven_out[3] = held("woven_out3", [P, WIDTHS[3] * PACK], BF16)
        weave_rows(nc.scalar.copy, woven_out[3][:, : PACK * P], y[3][:, :, :P])
        close_chunk(LAST)
        weave_rows(nc.vector.tensor_copy, woven_out[3][:, PACK * P :], y[3][:, :, P:])
        woven_out[LAST] = weave_out(nc.vector.tensor_copy, LAST, "woven_out4")
        quantize_out(LAST - 1)
        quantize_out(LAST)
        store_codes(slice(STARTS[LAST - 1], J))

        for q in range(QUADRANTS):
            queue = nc.sync if q % 2 == 0 else nc.scalar
            queue.dma_start(
                out=out_2[0, 4 * q : 4 * q + 4, :].bitcast(I32), in_=out_scale[32 * q : 32 * q + 4, :].bitcast(I32)
            )
